import numpy as np
import ml_dtypes


def mxq(x, axis, fmt="e4m3"):
    dtype, down = {"e4m3": (ml_dtypes.float8_e4m3fn, 7), "e5m2": (ml_dtypes.float8_e5m2, 14)}[fmt]
    v = np.moveaxis(np.asarray(x, np.float32).astype(ml_dtypes.bfloat16).astype(np.float64), axis, -1)
    blocks = v.reshape(v.shape[:-1] + (-1, 32))
    amax = np.abs(blocks).max(-1, keepdims=True)
    byte = np.maximum(np.where(amax > 0, np.frexp(amax)[1] - 1 + 127, 0) - down, 1)
    scale = np.exp2(byte - 127.0)
    codes = (blocks / scale).astype(np.float32).astype(dtype).astype(np.float64)
    return np.moveaxis((codes * scale).reshape(v.shape), -1, axis)


WIDE = False


def mx_kscale(k):
    if not WIDE:
        return np.ones(k)
    levels = np.array([10, -10, 5, -5, 0])
    if k % 512:
        return np.exp2(np.random.permutation(np.resize(levels, k // 32))).repeat(32)
    a = np.empty((k // 512, 16))
    for p in range(k // 512):
        a[p, :8] = np.random.permutation(np.resize(levels, 8))
        for g in range(8):
            far = levels[np.abs(levels - a[p, g]) >= 10]
            a[p, g + 8] = far[np.random.randint(len(far))]
    return np.exp2(a.ravel()).repeat(32)


BF16 = ml_dtypes.bfloat16


def bf(x):
    return np.asarray(x, np.float32).astype(BF16)


def f64(x):
    return np.asarray(x).astype(np.float64)


E2M1 = np.array([0.0, 0.5, 1.0, 1.5, 2.0, 3.0, 4.0, 6.0, -0.0, -0.5, -1.0, -1.5, -2.0, -3.0, -4.0, -6.0])


def pack_weight(w, fmt):
    k, n = w.shape
    w = f64(bf(w)).reshape(k // 32, 32, n)
    amax = np.abs(w).max(1)
    if fmt == "e4m3":
        byte = np.frexp(amax)[1] - 1 + 127 - 7
    else:
        mant, ex = np.frexp(amax / 6.0)
        byte = np.where(mant > 0.5, ex, ex - 1) + 127
    byte = np.clip(np.where(amax > 0, byte, 1), 1, 254)
    scaled = (w * np.exp2(127.0 - byte)[:, None, :]).reshape(k, n).astype(np.float32)
    by_word = np.ascontiguousarray(scaled.reshape(k // 512, 128, 4, n).transpose(0, 1, 3, 2))
    if fmt == "e4m3":
        words = by_word.astype(ml_dtypes.float8_e4m3fn).view(np.uint8)
    else:
        c = by_word.astype(ml_dtypes.float4_e2m1fn).view(np.uint8) & 0xF
        words = c[..., 0::2] | (c[..., 1::2] << 4)
    return np.ascontiguousarray(words), np.ascontiguousarray(byte.astype(np.uint8).reshape(k // 512, 16, n))


def unpack_weight(words, scales, fmt):
    g, p, n, _ = words.shape
    if fmt == "e4m3":
        vals = np.ascontiguousarray(words).view(ml_dtypes.float8_e4m3fn).astype(np.float64)
    else:
        nib = np.empty((g, p, n, 4), np.uint8)
        nib[..., 0::2] = words & 0xF
        nib[..., 1::2] = words >> 4
        vals = E2M1[nib]
    vals = vals * np.repeat(np.exp2(scales.astype(np.float64) - 127.0), 8, axis=1)[..., None]
    return vals.transpose(0, 1, 3, 2).reshape(g * 512, n)
def pack4(w):
    words, scales = pack_weight(w, "e2m1")
    return words.reshape(words.shape[0], 128, -1), scales


def unpack4(words, scales):
    return unpack_weight(words.reshape(words.shape[0], 128, -1, 2), scales, "e2m1")


def planes(Y):
    n, m = Y.shape
    b = f64(bf(Y)).reshape(n // 32, 32, m)
    amax = np.abs(b).max(1)
    byte = np.clip(np.where(amax > 0, np.frexp(amax)[1] - 1 + 127 - 7, 1), 1, 254)
    codes = (b * np.exp2(127.0 - byte)[:, None, :]).reshape(n, m).astype(np.float32).astype(ml_dtypes.float8_e4m3fn).view(np.uint8)
    words = codes.reshape(n // 512, 128, 4, m).transpose(0, 1, 3, 2)
    return np.ascontiguousarray(words), np.ascontiguousarray(byte.astype(np.uint8).reshape(n // 512, 16, m))


P, E, F, G, A = 2048, 1024, 1024, 8, 16
K = G * A
C = 2 * K
N = K - 1


def erf(a):
    c = np.clip(a, -6.0, 6.0)
    q = 2.0 * c * c
    term = c.copy()
    total = c.copy()
    for n in range(1, 150):
        term *= q
        term /= 2.0 * n + 1.0
        total += term
    return np.where(np.abs(a) > 6.0, np.sign(a), 2.0 / np.sqrt(np.pi) * np.exp(-c * c) * total)


def gelu_erf(v):
    return 0.5 * v * (1.0 + erf(v / np.sqrt(2.0)))


def softplus(v):
    return np.maximum(v, 0.0) + np.log(1.0 + np.exp(-np.abs(v)))


def log_binomial_stirling():
    eps = 1e-6
    n = float(N)
    k = np.arange(K, dtype=np.float64)
    lower = k + eps
    upper = n - k + eps
    return n * np.log(n) - lower * np.log(lower) - upper * np.log(upper)


def setup_inputs():
    s, t = mx_kscale(E), mx_kscale(F)
    x = bf(np.random.standard_normal((P, E)) * s)
    w1_words, w1_scales = pack4(np.random.standard_normal((E, F)) / np.sqrt(E) / s[:, None])
    b1 = bf(np.random.standard_normal(F) * 0.3)
    g = bf(np.random.standard_normal(F) * t)
    w_head_words, w_head_scales = pack4(np.random.standard_normal((F, C)) * 2.0 / np.sqrt(F) / t[:, None])
    w_q = bf(np.random.standard_normal(F) / np.sqrt(F) / t)
    return {
        "x": x,
        "w1_words": w1_words,
        "w1_scales": w1_scales,
        "b1": b1,
        "g": g,
        "w_head_words": w_head_words,
        "w_head_scales": w_head_scales,
        "w_q": w_q,
    }


def core(x, w1_words, w1_scales, b1, g, w_head_words, w_head_scales, w_q):
    rows = x.shape[0]

    h = gelu_erf((mxq(f64(x), 1, "e4m3") @ unpack4(w1_words, w1_scales)) + f64(b1)) * f64(g)

    y = softplus(mxq(h, 1, "e4m3") @ unpack4(w_head_words, w_head_scales))
    c = y[:, :K].reshape(rows, G, A)
    a = y[:, K:C].reshape(rows, G, A)

    dx = a[:, :, None, :] - c[:, :, :, None]
    pull = np.mean(dx / (1.0 + 2.0 * dx ** 2), axis=-1)
    c2 = (c + 2.0 * pull).reshape(rows, K)

    u = np.sum(h * f64(w_q)[None, :], axis=-1)

    lc = log_binomial_stirling()

    k = np.arange(K, dtype=np.float64)
    logits = (lc[None, :] + k[None, :] * u[:, None]) / 20.0
    e = np.exp(logits - logits.max(axis=-1, keepdims=True))
    p = e / e.sum(axis=-1, keepdims=True)

    return K * p * c2


def reference(x, w1_words, w1_scales, b1, g, w_head_words, w_head_scales, w_q):
    R_out = core(x, w1_words, w1_scales, b1, g, w_head_words, w_head_scales, w_q)
    words, scales = planes(R_out)
    return R_out, words, scales

@@ -1,0 +1,372 @@
+import math
+from contextlib import ExitStack
+
+import concourse.mybir as mybir
+from concourse.masks import make_identity
+
+F32 = mybir.dt.float32
+BF16 = mybir.dt.bfloat16
+I32 = mybir.dt.int32
+U32 = mybir.dt.uint32
+U8 = mybir.dt.uint8
+FP8X4 = mybir.dt.float8_e4m3fn_x4
+FP4X4 = mybir.dt.float4_e2m1fn_x4
+ACT = mybir.ActivationFunctionType
+ALU = mybir.AluOpType
+
+P = 128
+TOKENS, E, F, BINS = 2048, 1024, 1024, 128
+GROUPS, MEMBERS = 8, 16
+PACK = 4
+BLOCK = P * PACK
+BLOCKS = TOKENS // BLOCK
+TILES = TOKENS // P
+PASSES = E // BLOCK
+FT = F // P
+SHIFTS = 4
+CHUNKS = TILES * MEMBERS // SHIFTS
+BETA = 1.0 / math.sqrt(2.0)
+EPS = 1e-6
+TEMP = 20.0
+TRIALS = BINS - 1
+FLOPS = 2 * TOKENS * E * F + 2 * TOKENS * F * 2 * BINS
+
+X_BANKS = (0, 1)
+MM1_BANKS = (2, 3, 4)
+MM2_BANKS = (5, 6)
+U_BANK = 7
+DX_BANKS = (0, 1, 2, 3, 4)
+SUM_BANKS = (5, 6)
+SCALAR_SQUARE_EVERY = 11
+
+
+def tile_attractordepthbinhead_x2_kernel(tc, x, w1_words, w1_scales, b1, g, w_head_words, w_head_scales, w_q, out_0, out_1, out_2):
+    nc = tc.nc
+    with ExitStack() as ctx:
+        keep = ctx.enter_context(tc.tile_pool(name="keep", bufs=1))
+        work = ctx.enter_context(tc.tile_pool(name="work", bufs=2))
+        psum = ctx.enter_context(tc.psum_pool(name="psum", bufs=1))
+        ctx.enter_context(tc.manual_schedule())
+
+        def bank(b, name):
+            return psum.tile([P, BLOCK], F32, tag="bank%d" % b, name=name)
+
+        w1_raw = keep.tile([P, PASSES, 2 * F], U8, align_bytes=64)
+        s1_raw = keep.tile([P, PASSES, F], U8, align_bytes=64)
+        wh = keep.tile([P, PASSES, 4 * BINS], U8, align_bytes=64)
+        sh = keep.tile([P, PASSES, 2 * BINS], U8, align_bytes=64)
+        nc.vector.memset(s1_raw[:].bitcast(I32), 0)
+        nc.vector.memset(sh[:].bitcast(I32), 0)
+
+        x_raw = {}
+
+        def load_x(blk):
+            x_raw[blk] = work.tile([P, PACK, E], BF16, tag="x_raw", name="x_raw%d" % blk)
+            rows = x[blk * BLOCK:(blk + 1) * BLOCK, :].rearrange("(p t) e -> p t e", t=PACK)
+            for half in range(2):
+                nc.sync.dma_start(out=x_raw[blk][:, 2 * half:2 * half + 2, :], in_=rows[:, 2 * half:2 * half + 2, :])
+
+        nc.sync.dma_start(out=w1_raw[:].bitcast(I32), in_=w1_words.bitcast(I32).rearrange("g p n -> p g n"))
+        load_x(0)
+        for q in range(4):
+            nc.scalar.dma_start(out=s1_raw[32 * q:32 * q + 4].bitcast(I32), in_=w1_scales.bitcast(I32)[:, 4 * q:4 * q + 4, :].rearrange("g r n -> r g n"))
+        vec = {}
+        for name, src in (("b1", b1), ("g", g), ("wq", w_q)):
+            vec[name] = keep.tile([P, PASSES, PACK], BF16, name="vec_" + name)
+            nc.scalar.dma_start(out=vec[name][:], in_=src.rearrange("(a p t) -> p a t", a=PASSES, t=PACK))
+        load_x(1)
+        nc.sync.dma_start(out=wh[:].bitcast(I32), in_=w_head_words.bitcast(I32).rearrange("g p n -> p g n"))
+        for q in range(4):
+            nc.sync.dma_start(out=sh[32 * q:32 * q + 4].bitcast(I32), in_=w_head_scales.bitcast(I32)[:, 4 * q:4 * q + 4, :].rearrange("g r n -> r g n"))
+
+        ident = keep.tile([P, P], F32)
+        make_identity(nc, ident[:])
+        kvec = keep.tile([P, BINS], F32)
+        nc.gpsimd.iota(kvec[:], pattern=[[1, BINS]], base=0, channel_multiplier=0, allow_small_or_imprecise_dtypes=True)
+        lower = keep.tile([P, BINS], F32)
+        nc.gpsimd.tensor_scalar(out=lower[:], in0=kvec[:], scalar1=EPS, scalar2=1.0, op0=ALU.add, op1=ALU.mult)
+        bias1 = keep.tile([P, FT], F32)
+        nc.gpsimd.tensor_copy(out=bias1[:], in_=vec["b1"][:].rearrange("p a t -> p (a t)"))
+        gw = keep.tile([P, FT], F32)
+        nc.gpsimd.tensor_tensor(out=gw[:], in0=vec["g"][:].rearrange("p a t -> p (a t)"), in1=vec["wq"][:].rearrange("p a t -> p (a t)"), op=ALU.mult)
+        half_lc = keep.tile([P, BINS], F32)
+        nc.scalar.activation(out=half_lc[:], in_=lower[:], func=ACT.Ln, scale=1.0 / TRIALS)
+        warm = keep.tile([P, 1], F32)
+        nc.scalar.activation(out=warm[:], in_=lower[:, 0:1], func=ACT.Gelu)
+        lc = keep.tile([P, BINS], F32)
+
+        w1p = keep.tile([P, PASSES, 2 * F], U8, align_bytes=64)
+        s1p = keep.tile([P, PASSES, F], U8, align_bytes=64)
+
+        def permute_w1(a):
+            for kp in range(PASSES):
+                nc.vector.tensor_copy(
+                    out=w1p[:, kp, 2 * BLOCK * a:2 * BLOCK * (a + 1)].rearrange("p (t m b) -> p t m b", t=PACK, b=2),
+                    in_=w1_raw[:, kp, 2 * BLOCK * a:2 * BLOCK * (a + 1)].rearrange("p (m t b) -> p t m b", t=PACK, b=2))
+            nc.vector.tensor_copy(
+                out=s1p[:, :, BLOCK * a:BLOCK * (a + 1)].rearrange("p g (t m) -> p g t m", t=PACK),
+                in_=s1_raw[:, :, BLOCK * a:BLOCK * (a + 1)].rearrange("p g (m t) -> p g t m", t=PACK))
+
+        gel = keep.tile([P, BLOCKS, FT, BLOCK], F32)
+        soft = keep.tile([P, TILES, 2, BINS], F32)
+        relu = keep.tile([P, TILES, 2, BINS], F32)
+        ytab = keep.tile([P, TILES, 3, BINS], F32)
+        logit = keep.tile([P, TILES, BINS], F32)
+        res = keep.tile([P, TILES, BINS], F32)
+        slope = keep.tile([P, TILES], F32)
+        shift = keep.tile([P, TILES], F32)
+        total = keep.tile([P, TILES], F32)
+        norm = keep.tile([P, TILES], F32)
+        out_scales = keep.tile([P, BLOCKS, BINS], U8, align_bytes=64)
+        u_ps = psum.tile([P, TILES], F32, tag="bank%d" % U_BANK, name="u_ps")
+        xt, xg, xq, xs, z1, hg, hq, hs, z2 = {}, {}, {}, {}, {}, {}, {}, {}, {}
+
+        def turn_x(blk, b, banks=X_BANKS):
+            kp, tp = divmod(b, 2)
+            xt[blk, b] = bank(banks[b % len(banks)], "xt%d_%d" % (blk, b))
+            words = x_raw[blk][:].bitcast(F32)
+            for t in range(2):
+                for u in range(2):
+                    col = (2 * t + u) * P
+                    nc.tensor.transpose(xt[blk, b][:, col:col + P], words[:, 2 * tp + t, 2 * P * kp + u:2 * P * (kp + 1):2], ident[:])
+
+        def copy_x(blk, b):
+            kp, tp = divmod(b, 2)
+            if tp == 0:
+                xg[blk, kp] = work.tile([P, BLOCK * PACK], BF16, tag="xg", name="xg%d_%d" % (blk, kp), align_bytes=64)
+            dst = xg[blk, kp][:].bitcast(F32)[:, BLOCK * tp:BLOCK * (tp + 1)]
+            nc.scalar.copy(out=dst.rearrange("p (t r u) -> p t r u", t=2, u=2), in_=xt[blk, b][:].rearrange("p (t u r) -> p t r u", t=2, u=2))
+
+        def quant_x(blk, kp):
+            xq[blk, kp] = work.tile([P, BLOCK], U32, tag="xq", bufs=4, name="xq%d_%d" % (blk, kp), align_bytes=64)
+            xs[blk, kp] = work.tile([P, BLOCK], U8, tag="xs", bufs=4, name="xs%d_%d" % (blk, kp), align_bytes=64)
+            nc.vector.quantize_mx(out=xq[blk, kp][:].bitcast(FP8X4), scales=xs[blk, kp][:], in_=xg[blk, kp][:])
+
+        def mm1(blk, j):
+            z1[blk, j] = bank(MM1_BANKS[(FT * blk + j) % len(MM1_BANKS)], "z1_%d_%d" % (blk, j))
+            for kp in range(PASSES):
+                nc.tensor.matmul_mx(out=z1[blk, j][:], lhsT=w1p[:, kp, 2 * P * j:2 * P * (j + 1)].bitcast(FP4X4), lhsT_scale=s1p[:, kp, P * j:P * (j + 1)],
+                                    rhs=xq[blk, kp][:].bitcast(FP8X4), rhs_scale=xs[blk, kp][:], start=(kp == 0), stop=(kp == PASSES - 1))
+
+        def gelu(blk, j):
+            nc.scalar.activation(out=gel[:, blk, j, :], in_=z1[blk, j][:], func=ACT.Gelu, bias=bias1[:, j:j + 1])
+
+        def gain_h(blk, a):
+            hg[blk, a] = work.tile([P, BLOCK * PACK], BF16, tag="hg", name="hg%d_%d" % (blk, a), align_bytes=64)
+            nc.vector.tensor_tensor(
+                out=hg[blk, a][:].rearrange("p (c i t) -> p c t i", i=4, t=PACK),
+                in0=gel[:, blk, PACK * a:PACK * (a + 1), :].rearrange("p t (c i) -> p c t i", i=4),
+                in1=vec["g"][:, a, :].unsqueeze(1).unsqueeze(3).to_broadcast([P, BLOCK // 4, PACK, 4]), op=ALU.mult)
+
+        def quant_h(blk, a):
+            hq[blk, a] = work.tile([P, BLOCK], U32, tag="hq", bufs=3, name="hq%d_%d" % (blk, a), align_bytes=64)
+            hs[blk, a] = work.tile([P, BLOCK], U8, tag="hs", bufs=3, name="hs%d_%d" % (blk, a), align_bytes=64)
+            nc.vector.quantize_mx(out=hq[blk, a][:].bitcast(FP8X4), scales=hs[blk, a][:], in_=hg[blk, a][:])
+
+        def mm2(blk):
+            for tp in range(2):
+                z2[blk, tp] = bank(MM2_BANKS[tp], "z2_%d_%d" % (blk, tp))
+                for t in range(2):
+                    tok = slice(P * (2 * tp + t), P * (2 * tp + t + 1))
+                    for hf in range(2):
+                        col = (2 * t + hf) * BINS
+                        for a in range(PASSES):
+                            nc.tensor.matmul_mx(out=z2[blk, tp][:, col:col + BINS], lhsT=hq[blk, a][:, tok].bitcast(FP8X4), lhsT_scale=hs[blk, a][:, tok],
+                                                rhs=wh[:, a, 2 * BINS * hf:2 * BINS * (hf + 1)].bitcast(FP4X4), rhs_scale=sh[:, a, BINS * hf:BINS * (hf + 1)],
+                                                start=(a == 0), stop=(a == PASSES - 1))
+
+        def read_z2(blk, tp):
+            tl = slice(PACK * blk + 2 * tp, PACK * blk + 2 * tp + 2)
+            src = z2[blk, tp][:].rearrange("p (s q i) -> p s i q", q=GROUPS, i=MEMBERS)
+            nc.scalar.activation(out=soft[:, tl].rearrange("p t h (i q) -> p (t h) i q", q=GROUPS), in_=src, func=ACT.Abs)
+            nc.vector.tensor_scalar(out=relu[:, tl].rearrange("p t h (i q) -> p (t h) i q", q=GROUPS), in0=src, scalar1=0.0, scalar2=None, op0=ALU.max)
+
+        def soft_block(blk):
+            return soft[:, PACK * blk:PACK * (blk + 1)].rearrange("p t h m -> p (t h m)")
+
+        def tanh_block(blk):
+            nc.scalar.activation(out=soft_block(blk), in_=soft_block(blk), func=ACT.Tanh, scale=0.5)
+
+        def ln_block(blk):
+            nc.scalar.activation(out=soft_block(blk), in_=soft_block(blk), func=ACT.Ln, scale=0.5, bias=0.5)
+
+        def finish_y(blk):
+            tl = slice(PACK * blk, PACK * (blk + 1))
+            nc.vector.scalar_tensor_tensor(out=ytab[:, tl, 0, :], in0=soft[:, tl, 0, :], scalar=BETA, in1=relu[:, tl, 0, :], op0=ALU.add, op1=ALU.subtract)
+            nc.vector.tensor_tensor(out=ytab[:, tl, 1:3, :], in0=relu[:, tl, 1:2, :].to_broadcast([P, PACK, 2, BINS]),
+                                    in1=soft[:, tl, 1:2, :].to_broadcast([P, PACK, 2, BINS]), op=ALU.subtract)
+
+        def sum_u(tile):
+            blk, t = divmod(tile, PACK)
+            for j in range(FT):
+                nc.tensor.matmul(out=u_ps[:, tile:tile + 1], lhsT=gel[:, blk, j, P * t:P * (t + 1)], rhs=gw[:, j:j + 1], start=(j == 0), stop=(j == FT - 1))
+
+        dx, pair, acc = {}, {}, {}
+
+        def make_dx(n):
+            tile, part = divmod(n, MEMBERS // SHIFTS)
+            dx[n] = bank(DX_BANKS[n % len(DX_BANKS)], "dx%d" % n)
+            row = ytab[:, tile].rearrange("p s m -> p (s m)")
+            for k in range(SHIFTS):
+                start = BINS + GROUPS * (SHIFTS * part + k)
+                nc.tensor.matmul(out=dx[n][:, P * k:P * (k + 1)], lhsT=row[:, start:start + BINS], rhs=ident[:], start=True, stop=False, is_transpose=True)
+                nc.tensor.matmul(out=dx[n][:, P * k:P * (k + 1)], lhsT=row[:, 0:BINS], rhs=ident[:], start=False, stop=True, is_transpose=True)
+
+        def square_dx(n):
+            pair[n] = work.tile([P, BLOCK], F32, tag="pair", bufs=6, name="pair%d" % n)
+            nc.scalar.activation(out=pair[n][:], in_=dx[n][:], func=ACT.Square, bias=-BETA)
+
+        def rsqrt(n):
+            nc.scalar.activation(out=pair[n][:], in_=pair[n][:], func=ACT.Abs_reciprocal_sqrt, scale=2.0, bias=1.0)
+
+        def weigh(n):
+            nc.vector.tensor_tensor(out=pair[n][:], in0=dx[n][:], in1=pair[n][:], op=ALU.mult)
+
+        def square_e(n):
+            if n % SCALAR_SQUARE_EVERY == SCALAR_SQUARE_EVERY - 1:
+                nc.scalar.activation(out=pair[n][:], in_=pair[n][:], func=ACT.Square)
+            else:
+                nc.vector.tensor_tensor(out=pair[n][:], in0=pair[n][:], in1=pair[n][:], op=ALU.mult)
+
+        def reduce_e(n):
+            tile, part = divmod(n, MEMBERS // SHIFTS)
+            if part == 0:
+                acc[tile] = psum.tile([P, BINS], F32, tag="bank%d" % SUM_BANKS[tile % 2], name="acc%d" % tile)
+            for k in range(SHIFTS):
+                s = SHIFTS * part + k
+                nc.tensor.matmul(out=acc[tile][:], lhsT=pair[n][:, P * k:P * (k + 1)], rhs=ident[:], start=(s == 0), stop=(s == MEMBERS - 1), is_transpose=True)
+
+        def centres(tile):
+            nc.vector.scalar_tensor_tensor(out=res[:, tile, :].rearrange("p (q i) -> p q i", i=MEMBERS), in0=acc[tile][:].rearrange("p (i q) -> p q i", q=GROUPS),
+                                           scalar=2.0 * BETA / MEMBERS, in1=ytab[:, tile, 0, :].rearrange("p (i q) -> p q i", q=GROUPS), op0=ALU.mult, op1=ALU.subtract)
+
+        def slopes():
+            nc.vector.tensor_scalar(out=slope[:], in0=u_ps[:], scalar1=1.0 / TEMP, scalar2=None, op0=ALU.mult)
+            nc.vector.tensor_scalar(out=shift[:], in0=u_ps[:], scalar1=0.0, scalar2=-TRIALS / TEMP, op0=ALU.max, op1=ALU.mult)
+
+        def make_logits(tile):
+            nc.vector.scalar_tensor_tensor(out=logit[:, tile, :], in0=kvec[:], scalar=slope[:, tile:tile + 1], in1=lc[:], op0=ALU.mult, op1=ALU.add)
+
+        def exp_tile(tile):
+            nc.scalar.activation(out=logit[:, tile, :], in_=logit[:, tile, :], func=ACT.Exp, bias=shift[:, tile:tile + 1], accum_out=total[:, tile:tile + 1])
+
+        permute_w1(0)
+        for b in range(4):
+            turn_x(0, b, X_BANKS + MM2_BANKS)
+        load_x(2)
+        for b in range(4):
+            copy_x(0, b)
+            if b % 2 == 1:
+                quant_x(0, b // 2)
+        permute_w1(1)
+        nc.vector.scalar_tensor_tensor(out=half_lc[:], in0=lower[:], scalar=-1.0 / TEMP, in1=half_lc[:], op0=ALU.mult, op1=ALU.mult)
+        for j in range(3):
+            mm1(0, j)
+        nc.vector.tensor_tensor(out=lc[:], in0=half_lc[:], in1=half_lc[:, ::-1], op=ALU.add)
+        u_next = 0
+        for blk in range(BLOCKS):
+            more, prev = blk + 1 < BLOCKS, blk > 0
+            if prev:
+                gain_h(blk - 1, 1)
+            if more:
+                turn_x(blk + 1, 0)
+                turn_x(blk + 1, 1)
+            gelu(blk, 0)
+            mm1(blk, 3)
+            gelu(blk, 1)
+            mm1(blk, 4)
+            if more:
+                copy_x(blk + 1, 0)
+                copy_x(blk + 1, 1)
+                quant_x(blk + 1, 0)
+            if prev:
+                quant_h(blk - 1, 1)
+            if more:
+                turn_x(blk + 1, 2)
+                turn_x(blk + 1, 3)
+                if blk + 3 < BLOCKS:
+                    load_x(blk + 3)
+            gelu(blk, 2)
+            mm1(blk, 5)
+            gelu(blk, 3)
+            gain_h(blk, 0)
+            if prev:
+                mm2(blk - 1)
+            mm1(blk, 6)
+            if more:
+                copy_x(blk + 1, 2)
+                copy_x(blk + 1, 3)
+                quant_x(blk + 1, 1)
+            quant_h(blk, 0)
+            gelu(blk, 4)
+            mm1(blk, 7)
+            if prev:
+                sum_u(u_next)
+                u_next += 1
+                read_z2(blk - 1, 0)
+                read_z2(blk - 1, 1)
+            for j in range(5, 8):
+                gelu(blk, j)
+                if more:
+                    mm1(blk + 1, j - 5)
+            if prev:
+                tanh_block(blk - 1)
+        last = BLOCKS - 1
+        gain_h(last, 1)
+        for k in range(2):
+            sum_u(u_next)
+            u_next += 1
+        quant_h(last, 1)
+        mm2(last)
+        read_z2(last, 0)
+        read_z2(last, 1)
+        tanh_block(last)
+        for k in range(3):
+            sum_u(u_next)
+            u_next += 1
+        for blk in range(BLOCKS):
+            ln_block(blk)
+            finish_y(blk)
+
+        make_dx(0)
+        logits_next = 0
+        for k in range(CHUNKS + 5):
+            if k + 1 < CHUNKS:
+                make_dx(k + 1)
+            if k < CHUNKS:
+                square_dx(k)
+            if 0 <= k - 1 < CHUNKS:
+                rsqrt(k - 1)
+            if 0 <= k - 2 < CHUNKS:
+                weigh(k - 2)
+            if 0 <= k - 3 < CHUNKS:
+                square_e(k - 3)
+            if 0 <= k - 4 < CHUNKS:
+                reduce_e(k - 4)
+            if k >= 5 and (k - 5) % 4 == 3:
+                centres((k - 5) // 4)
+            if k % 4 == 1 and u_next < TILES:
+                sum_u(u_next)
+                u_next += 1
+            if k == 40:
+                slopes()
+            if k > 41 and logits_next < TILES:
+                make_logits(logits_next)
+                logits_next += 1
+
+        for blk in range(BLOCKS):
+            tl = slice(PACK * blk, PACK * (blk + 1))
+            for tile in range(PACK * blk, PACK * (blk + 1)):
+                exp_tile(tile)
+            nc.vector.tensor_scalar(out=total[:, tl], in0=total[:, tl], scalar1=1.0 / BINS, scalar2=None, op0=ALU.mult)
+            nc.vector.reciprocal(out=norm[:, tl], in_=total[:, tl])
+            for tile in range(PACK * blk, PACK * (blk + 1)):
+                nc.vector.scalar_tensor_tensor(out=res[:, tile, :], in0=res[:, tile, :], scalar=norm[:, tile:tile + 1], in1=logit[:, tile, :], op0=ALU.mult, op1=ALU.mult)
+            nc.sync.dma_start(out=out_0[BLOCK * blk:BLOCK * (blk + 1), :].rearrange("(p t) m -> p t m", t=PACK), in_=res[:, tl, :])
+            rounded = work.tile([P, BINS * PACK], BF16, tag="rounded", name="rounded%d" % blk, align_bytes=64)
+            nc.vector.tensor_copy(out=rounded[:].rearrange("p (m t) -> p m t", t=PACK), in_=res[:, tl, :].rearrange("p t m -> p m t"))
+            codes = work.tile([P, BINS], U32, tag="codes", bufs=4, name="codes%d" % blk, align_bytes=64)
+            nc.vector.quantize_mx(out=codes[:].bitcast(FP8X4), scales=out_scales[:, blk, :], in_=rounded[:])
+            nc.sync.dma_start(out=out_1[blk].rearrange("p m t -> p (m t)").bitcast(I32), in_=codes[:].bitcast(I32))
+        for q in range(4):
+            nc.scalar.dma_start(out=out_2.bitcast(I32)[:, 4 * q:4 * q + 4, :].rearrange("g r m -> r g m"), in_=out_scales[32 * q:32 * q + 4].bitcast(I32))

@@ -37,7 +37,7 @@ MM2_BANKS = (5, 6)
 U_BANK = 7
 DX_BANKS = (0, 1, 2, 3, 4)
 SUM_BANKS = (5, 6)
-SCALAR_SQUARE_EVERY = 11
+SCALAR_SQUARE_EVERY = 8
 
 
 def tile_attractordepthbinhead_x2_kernel(tc, x, w1_words, w1_scales, b1, g, w_head_words, w_head_scales, w_q, out_0, out_1, out_2):
@@ -118,7 +118,10 @@ def tile_attractordepthbinhead_x2_kernel(tc, x, w1_words, w1_scales, b1, g, w_he
         total = keep.tile([P, TILES], F32)
         norm = keep.tile([P, TILES], F32)
         out_scales = keep.tile([P, BLOCKS, BINS], U8, align_bytes=64)
-        u_ps = psum.tile([P, TILES], F32, tag="bank%d" % U_BANK, name="u_ps")
+        u_sum = keep.tile([P, TILES], F32)
+        idle = keep.tile([P, P], BF16)
+        nc.gpsimd.memset(idle[:], 0.0)
+        u_ps = {}
         xt, xg, xq, xs, z1, hg, hq, hs, z2 = {}, {}, {}, {}, {}, {}, {}, {}, {}
 
         def turn_x(blk, b, banks=X_BANKS):
@@ -154,9 +157,9 @@ def tile_attractordepthbinhead_x2_kernel(tc, x, w1_words, w1_scales, b1, g, w_he
         def gain_h(blk, a):
             hg[blk, a] = work.tile([P, BLOCK * PACK], BF16, tag="hg", name="hg%d_%d" % (blk, a), align_bytes=64)
             nc.vector.tensor_tensor(
-                out=hg[blk, a][:].rearrange("p (c i t) -> p c t i", i=4, t=PACK),
-                in0=gel[:, blk, PACK * a:PACK * (a + 1), :].rearrange("p t (c i) -> p c t i", i=4),
-                in1=vec["g"][:, a, :].unsqueeze(1).unsqueeze(3).to_broadcast([P, BLOCK // 4, PACK, 4]), op=ALU.mult)
+                out=hg[blk, a][:].rearrange("p (n t) -> p n t", t=PACK),
+                in0=gel[:, blk, PACK * a:PACK * (a + 1), :].rearrange("p t n -> p n t"),
+                in1=vec["g"][:, a, :].unsqueeze(1).to_broadcast([P, BLOCK, PACK]), op=ALU.mult)
 
         def quant_h(blk, a):
             hq[blk, a] = work.tile([P, BLOCK], U32, tag="hq", bufs=3, name="hq%d_%d" % (blk, a), align_bytes=64)
@@ -196,10 +199,18 @@ def tile_attractordepthbinhead_x2_kernel(tc, x, w1_words, w1_scales, b1, g, w_he
             nc.vector.tensor_tensor(out=ytab[:, tl, 1:3, :], in0=relu[:, tl, 1:2, :].to_broadcast([P, PACK, 2, BINS]),
                                     in1=soft[:, tl, 1:2, :].to_broadcast([P, PACK, 2, BINS]), op=ALU.subtract)
 
-        def sum_u(tile):
+        def weigh_u(blk, j):
+            nc.vector.tensor_scalar(out=gel[:, blk, j, :], in0=gel[:, blk, j, :], scalar1=gw[:, j:j + 1], scalar2=None, op0=ALU.mult)
+
+        def turn_u(tile):
             blk, t = divmod(tile, PACK)
+            if t == 0:
+                u_ps[blk] = bank(U_BANK, "u_ps%d" % blk)
             for j in range(FT):
-                nc.tensor.matmul(out=u_ps[:, tile:tile + 1], lhsT=gel[:, blk, j, P * t:P * (t + 1)], rhs=gw[:, j:j + 1], start=(j == 0), stop=(j == FT - 1))
+                nc.tensor.matmul(out=u_ps[blk][:, P * t:P * (t + 1)], lhsT=gel[:, blk, j, P * t:P * (t + 1)], rhs=ident[:], start=(j == 0), stop=(j == FT - 1), is_transpose=True)
+
+        def sum_u(blk):
+            nc.vector.tensor_reduce(out=u_sum[:, PACK * blk:PACK * (blk + 1)], in_=u_ps[blk][:].rearrange("p (t f) -> p t f", t=PACK), axis=mybir.AxisListType.X, op=ALU.add)
 
         dx, pair, acc = {}, {}, {}
 
@@ -207,6 +218,12 @@ def tile_attractordepthbinhead_x2_kernel(tc, x, w1_words, w1_scales, b1, g, w_he
             tile, part = divmod(n, MEMBERS // SHIFTS)
             dx[n] = bank(DX_BANKS[n % len(DX_BANKS)], "dx%d" % n)
             row = ytab[:, tile].rearrange("p s m -> p (s m)")
+            if n in (1, 2):
+                nc.tensor.matmul(out=dx[n][:], lhsT=ident[:], rhs=relu[:, 0:2].rearrange("p t h m -> p (t h m)"), start=True, stop=True)
+            elif n % 8 == 0 and n > 0:
+                nc.tensor.matmul(out=dx[n][:, 0:2 * P], lhsT=ident[:], rhs=relu[:, 0].rearrange("p h m -> p (h m)"), start=True, stop=True)
+            elif n > 0:
+                nc.tensor.matmul(out=dx[n][:, 0:P], lhsT=idle[:], rhs=idle[:], start=True, stop=True)
             for k in range(SHIFTS):
                 start = BINS + GROUPS * (SHIFTS * part + k)
                 nc.tensor.matmul(out=dx[n][:, P * k:P * (k + 1)], lhsT=row[:, start:start + BINS], rhs=ident[:], start=True, stop=False, is_transpose=True)
@@ -241,8 +258,8 @@ def tile_attractordepthbinhead_x2_kernel(tc, x, w1_words, w1_scales, b1, g, w_he
                                            scalar=2.0 * BETA / MEMBERS, in1=ytab[:, tile, 0, :].rearrange("p (i q) -> p q i", q=GROUPS), op0=ALU.mult, op1=ALU.subtract)
 
         def slopes():
-            nc.vector.tensor_scalar(out=slope[:], in0=u_ps[:], scalar1=1.0 / TEMP, scalar2=None, op0=ALU.mult)
-            nc.vector.tensor_scalar(out=shift[:], in0=u_ps[:], scalar1=0.0, scalar2=-TRIALS / TEMP, op0=ALU.max, op1=ALU.mult)
+            nc.vector.tensor_scalar(out=slope[:], in0=u_sum[:], scalar1=1.0 / TEMP, scalar2=None, op0=ALU.mult)
+            nc.vector.tensor_scalar(out=shift[:], in0=u_sum[:], scalar1=0.0, scalar2=-TRIALS / TEMP, op0=ALU.max, op1=ALU.mult)
 
         def make_logits(tile):
             nc.vector.scalar_tensor_tensor(out=logit[:, tile, :], in0=kvec[:], scalar=slope[:, tile:tile + 1], in1=lc[:], op0=ALU.mult, op1=ALU.add)
@@ -263,7 +280,6 @@ def tile_attractordepthbinhead_x2_kernel(tc, x, w1_words, w1_scales, b1, g, w_he
         for j in range(3):
             mm1(0, j)
         nc.vector.tensor_tensor(out=lc[:], in0=half_lc[:], in1=half_lc[:, ::-1], op=ALU.add)
-        u_next = 0
         for blk in range(BLOCKS):
             more, prev = blk + 1 < BLOCKS, blk > 0
             if prev:
@@ -301,10 +317,10 @@ def tile_attractordepthbinhead_x2_kernel(tc, x, w1_words, w1_scales, b1, g, w_he
             gelu(blk, 4)
             mm1(blk, 7)
             if prev:
-                sum_u(u_next)
-                u_next += 1
                 read_z2(blk - 1, 0)
                 read_z2(blk - 1, 1)
+            for j in range(PACK):
+                weigh_u(blk, j)
             for j in range(5, 8):
                 gelu(blk, j)
                 if more:
@@ -313,20 +329,25 @@ def tile_attractordepthbinhead_x2_kernel(tc, x, w1_words, w1_scales, b1, g, w_he
                 tanh_block(blk - 1)
         last = BLOCKS - 1
         gain_h(last, 1)
-        for k in range(2):
-            sum_u(u_next)
-            u_next += 1
+        weigh_u(0, 4)
         quant_h(last, 1)
         mm2(last)
+        for j in range(5, FT):
+            weigh_u(0, j)
         read_z2(last, 0)
         read_z2(last, 1)
         tanh_block(last)
-        for k in range(3):
-            sum_u(u_next)
-            u_next += 1
+        for j in range(PACK, FT):
+            weigh_u(1, j)
+        for tile in range(PACK):
+            turn_u(tile)
+        sum_u(0)
+        for tile in range(PACK, 2 * PACK):
+            turn_u(tile)
         for blk in range(BLOCKS):
             ln_block(blk)
             finish_y(blk)
+        sum_u(1)
 
         make_dx(0)
         logits_next = 0
@@ -345,9 +366,12 @@ def tile_attractordepthbinhead_x2_kernel(tc, x, w1_words, w1_scales, b1, g, w_he
                 reduce_e(k - 4)
             if k >= 5 and (k - 5) % 4 == 3:
                 centres((k - 5) // 4)
-            if k % 4 == 1 and u_next < TILES:
-                sum_u(u_next)
-                u_next += 1
+            if k % 2 == 0 and k < 16:
+                weigh_u(2 + k // 8, PACK + (k // 2) % PACK)
+            if k % 3 == 0 and 9 <= k < 33:
+                turn_u(2 * PACK + (k - 9) // 3)
+            if k == 20 or k == 33:
+                sum_u(2 if k == 20 else 3)
             if k == 40:
                 slopes()
             if k > 41 and logits_next < TILES:

@@ -34,7 +34,7 @@ FLOPS = 2 * TOKENS * E * F + 2 * TOKENS * F * 2 * BINS
 X_BANKS = (0, 1)
 MM1_BANKS = (2, 3, 4)
 MM2_BANKS = (5, 6)
-U_BANK = 7
+U_BANKS = (7, 4, 3, 7)
 DX_BANKS = (0, 1, 2, 3, 4)
 SUM_BANKS = (5, 6)
 SCALAR_SQUARE_EVERY = 8
@@ -119,8 +119,6 @@ def tile_attractordepthbinhead_x2_kernel(tc, x, w1_words, w1_scales, b1, g, w_he
         norm = keep.tile([P, TILES], F32)
         out_scales = keep.tile([P, BLOCKS, BINS], U8, align_bytes=64)
         u_sum = keep.tile([P, TILES], F32)
-        idle = keep.tile([P, P], BF16)
-        nc.gpsimd.memset(idle[:], 0.0)
         u_ps = {}
         xt, xg, xq, xs, z1, hg, hq, hs, z2 = {}, {}, {}, {}, {}, {}, {}, {}, {}
 
@@ -205,32 +203,27 @@ def tile_attractordepthbinhead_x2_kernel(tc, x, w1_words, w1_scales, b1, g, w_he
         def turn_u(tile):
             blk, t = divmod(tile, PACK)
             if t == 0:
-                u_ps[blk] = bank(U_BANK, "u_ps%d" % blk)
+                u_ps[blk] = bank(U_BANKS[blk], "u_ps%d" % blk)
             for j in range(FT):
-                nc.tensor.matmul(out=u_ps[blk][:, P * t:P * (t + 1)], lhsT=gel[:, blk, j, P * t:P * (t + 1)], rhs=ident[:], start=(j == 0), stop=(j == FT - 1), is_transpose=True)
+                nc.tensor.matmul(out=u_ps[blk][:, P * t:P * (t + 1)], lhsT=gel[:, blk, j, P * t:P * (t + 1)], rhs=ident[:], start=(j == 0), stop=(j == FT - 1), is_transpose=not (blk in (1, 2) and j % 4 == 0))
 
         def sum_u(blk):
             nc.vector.tensor_reduce(out=u_sum[:, PACK * blk:PACK * (blk + 1)], in_=u_ps[blk][:].rearrange("p (t f) -> p t f", t=PACK), axis=mybir.AxisListType.X, op=ALU.add)
 
         dx, pair, acc = {}, {}, {}
 
-        def make_dx(n):
+        def make_dx(n, k):
             tile, part = divmod(n, MEMBERS // SHIFTS)
-            dx[n] = bank(DX_BANKS[n % len(DX_BANKS)], "dx%d" % n)
+            if k == 0:
+                dx[n] = bank(DX_BANKS[n % len(DX_BANKS)], "dx%d" % n)
             row = ytab[:, tile].rearrange("p s m -> p (s m)")
-            if n in (1, 2):
-                nc.tensor.matmul(out=dx[n][:], lhsT=ident[:], rhs=relu[:, 0:2].rearrange("p t h m -> p (t h m)"), start=True, stop=True)
-            elif n % 8 == 0 and n > 0:
-                nc.tensor.matmul(out=dx[n][:, 0:2 * P], lhsT=ident[:], rhs=relu[:, 0].rearrange("p h m -> p (h m)"), start=True, stop=True)
-            elif n > 0:
-                nc.tensor.matmul(out=dx[n][:, 0:P], lhsT=idle[:], rhs=idle[:], start=True, stop=True)
-            for k in range(SHIFTS):
-                start = BINS + GROUPS * (SHIFTS * part + k)
-                nc.tensor.matmul(out=dx[n][:, P * k:P * (k + 1)], lhsT=row[:, start:start + BINS], rhs=ident[:], start=True, stop=False, is_transpose=True)
-                nc.tensor.matmul(out=dx[n][:, P * k:P * (k + 1)], lhsT=row[:, 0:BINS], rhs=ident[:], start=False, stop=True, is_transpose=True)
+            start = BINS + GROUPS * (SHIFTS * part + k)
+            plain = k in ((0, 2) if n < 6 else (0, 3) if n % 2 == 0 else (1,))
+            nc.tensor.matmul(out=dx[n][:, P * k:P * (k + 1)], lhsT=row[:, start:start + BINS], rhs=ident[:], start=True, stop=False, is_transpose=True)
+            nc.tensor.matmul(out=dx[n][:, P * k:P * (k + 1)], lhsT=row[:, 0:BINS], rhs=ident[:], start=False, stop=True, is_transpose=not plain)
 
         def square_dx(n):
-            pair[n] = work.tile([P, BLOCK], F32, tag="pair", bufs=6, name="pair%d" % n)
+            pair[n] = work.tile([P, BLOCK], F32, tag="pair", bufs=7, name="pair%d" % n)
             nc.scalar.activation(out=pair[n][:], in_=dx[n][:], func=ACT.Square, bias=-BETA)
 
         def rsqrt(n):
@@ -240,18 +233,17 @@ def tile_attractordepthbinhead_x2_kernel(tc, x, w1_words, w1_scales, b1, g, w_he
             nc.vector.tensor_tensor(out=pair[n][:], in0=dx[n][:], in1=pair[n][:], op=ALU.mult)
 
         def square_e(n):
-            if n % SCALAR_SQUARE_EVERY == SCALAR_SQUARE_EVERY - 1:
+            if n % SCALAR_SQUARE_EVERY == 3:
                 nc.scalar.activation(out=pair[n][:], in_=pair[n][:], func=ACT.Square)
             else:
                 nc.vector.tensor_tensor(out=pair[n][:], in0=pair[n][:], in1=pair[n][:], op=ALU.mult)
 
-        def reduce_e(n):
+        def reduce_e(n, k):
             tile, part = divmod(n, MEMBERS // SHIFTS)
-            if part == 0:
+            s = SHIFTS * part + k
+            if s == 0:
                 acc[tile] = psum.tile([P, BINS], F32, tag="bank%d" % SUM_BANKS[tile % 2], name="acc%d" % tile)
-            for k in range(SHIFTS):
-                s = SHIFTS * part + k
-                nc.tensor.matmul(out=acc[tile][:], lhsT=pair[n][:, P * k:P * (k + 1)], rhs=ident[:], start=(s == 0), stop=(s == MEMBERS - 1), is_transpose=True)
+            nc.tensor.matmul(out=acc[tile][:], lhsT=pair[n][:, P * k:P * (k + 1)], rhs=ident[:], start=(s == 0), stop=(s == MEMBERS - 1), is_transpose=True)
 
         def centres(tile):
             nc.vector.scalar_tensor_tensor(out=res[:, tile, :].rearrange("p (q i) -> p q i", i=MEMBERS), in0=acc[tile][:].rearrange("p (i q) -> p q i", q=GROUPS),
@@ -320,7 +312,7 @@ def tile_attractordepthbinhead_x2_kernel(tc, x, w1_words, w1_scales, b1, g, w_he
                 read_z2(blk - 1, 0)
                 read_z2(blk - 1, 1)
             for j in range(PACK):
-                weigh_u(blk, j)
+                weigh_u(blk // 2, PACK * (blk % 2) + j)
             for j in range(5, 8):
                 gelu(blk, j)
                 if more:
@@ -329,31 +321,39 @@ def tile_attractordepthbinhead_x2_kernel(tc, x, w1_words, w1_scales, b1, g, w_he
                 tanh_block(blk - 1)
         last = BLOCKS - 1
         gain_h(last, 1)
-        weigh_u(0, 4)
+        for tile in range(PACK):
+            turn_u(tile)
+        weigh_u(2, 0)
         quant_h(last, 1)
         mm2(last)
-        for j in range(5, FT):
-            weigh_u(0, j)
+        for j in range(1, 4):
+            weigh_u(2, j)
         read_z2(last, 0)
         read_z2(last, 1)
         tanh_block(last)
-        for j in range(PACK, FT):
-            weigh_u(1, j)
-        for tile in range(PACK):
-            turn_u(tile)
-        sum_u(0)
         for tile in range(PACK, 2 * PACK):
             turn_u(tile)
+        for j in range(PACK, FT):
+            weigh_u(2, j)
+        for tile in range(2 * PACK, 3 * PACK):
+            turn_u(tile)
+        sum_u(0)
+        sum_u(1)
         for blk in range(BLOCKS):
             ln_block(blk)
             finish_y(blk)
-        sum_u(1)
+            if blk == 0:
+                sum_u(2)
 
-        make_dx(0)
+        for k in range(SHIFTS):
+            make_dx(0, k)
         logits_next = 0
-        for k in range(CHUNKS + 5):
-            if k + 1 < CHUNKS:
-                make_dx(k + 1)
+        for k in range(CHUNKS + 6):
+            for c in range(SHIFTS):
+                if k + 1 < CHUNKS:
+                    make_dx(k + 1, c)
+                if 0 <= k - 5 < CHUNKS:
+                    reduce_e(k - 5, c)
             if k < CHUNKS:
                 square_dx(k)
             if 0 <= k - 1 < CHUNKS:
@@ -362,35 +362,55 @@ def tile_attractordepthbinhead_x2_kernel(tc, x, w1_words, w1_scales, b1, g, w_he
                 weigh(k - 2)
             if 0 <= k - 3 < CHUNKS:
                 square_e(k - 3)
-            if 0 <= k - 4 < CHUNKS:
-                reduce_e(k - 4)
-            if k >= 5 and (k - 5) % 4 == 3:
-                centres((k - 5) // 4)
+            if k >= 6 and (k - 6) % 4 == 3:
+                centres((k - 6) // 4)
             if k % 2 == 0 and k < 16:
-                weigh_u(2 + k // 8, PACK + (k // 2) % PACK)
-            if k % 3 == 0 and 9 <= k < 33:
-                turn_u(2 * PACK + (k - 9) // 3)
-            if k == 20 or k == 33:
-                sum_u(2 if k == 20 else 3)
+                weigh_u(last, k // 2)
+            if k % 4 == 0 and 16 <= k < 32:
+                turn_u(3 * PACK + (k - 16) // 4)
+            if k == 33:
+                sum_u(last)
             if k == 40:
                 slopes()
             if k > 41 and logits_next < TILES:
                 make_logits(logits_next)
                 logits_next += 1
 
-        for blk in range(BLOCKS):
-            tl = slice(PACK * blk, PACK * (blk + 1))
-            for tile in range(PACK * blk, PACK * (blk + 1)):
-                exp_tile(tile)
-            nc.vector.tensor_scalar(out=total[:, tl], in0=total[:, tl], scalar1=1.0 / BINS, scalar2=None, op0=ALU.mult)
-            nc.vector.reciprocal(out=norm[:, tl], in_=total[:, tl])
+        rounded = {}
+
+        def tiles_of(blk):
+            return slice(PACK * blk, PACK * (blk + 1))
+
+        def scale_total(blk):
+            nc.vector.tensor_scalar(out=total[:, tiles_of(blk)], in0=total[:, tiles_of(blk)], scalar1=1.0 / BINS, scalar2=None, op0=ALU.mult)
+
+        def invert_total(blk):
+            nc.vector.reciprocal(out=norm[:, tiles_of(blk)], in_=total[:, tiles_of(blk)])
+
+        def finish(blk):
             for tile in range(PACK * blk, PACK * (blk + 1)):
                 nc.vector.scalar_tensor_tensor(out=res[:, tile, :], in0=res[:, tile, :], scalar=norm[:, tile:tile + 1], in1=logit[:, tile, :], op0=ALU.mult, op1=ALU.mult)
-            nc.sync.dma_start(out=out_0[BLOCK * blk:BLOCK * (blk + 1), :].rearrange("(p t) m -> p t m", t=PACK), in_=res[:, tl, :])
-            rounded = work.tile([P, BINS * PACK], BF16, tag="rounded", name="rounded%d" % blk, align_bytes=64)
-            nc.vector.tensor_copy(out=rounded[:].rearrange("p (m t) -> p m t", t=PACK), in_=res[:, tl, :].rearrange("p t m -> p m t"))
+            nc.sync.dma_start(out=out_0[BLOCK * blk:BLOCK * (blk + 1), :].rearrange("(p t) m -> p t m", t=PACK), in_=res[:, tiles_of(blk), :])
+            rounded[blk] = work.tile([P, BINS * PACK], BF16, tag="rounded", bufs=4, name="rounded%d" % blk, align_bytes=64)
+            nc.scalar.copy(out=rounded[blk][:].rearrange("p (m t) -> p m t", t=PACK), in_=res[:, tiles_of(blk), :].rearrange("p t m -> p m t"))
+
+        def planes(blk):
             codes = work.tile([P, BINS], U32, tag="codes", bufs=4, name="codes%d" % blk, align_bytes=64)
-            nc.vector.quantize_mx(out=codes[:].bitcast(FP8X4), scales=out_scales[:, blk, :], in_=rounded[:])
+            nc.vector.quantize_mx(out=codes[:].bitcast(FP8X4), scales=out_scales[:, blk, :], in_=rounded[blk][:])
             nc.sync.dma_start(out=out_1[blk].rearrange("p m t -> p (m t)").bitcast(I32), in_=codes[:].bitcast(I32))
+
+        for tile in range(TILES):
+            exp_tile(tile)
+        scale_total(0)
+        invert_total(0)
+        for blk in range(BLOCKS):
+            if blk + 1 < BLOCKS:
+                scale_total(blk + 1)
+            finish(blk)
+            if blk + 1 < BLOCKS:
+                invert_total(blk + 1)
+            if blk > 0:
+                planes(blk - 1)
+        planes(last)
         for q in range(4):
             nc.scalar.dma_start(out=out_2.bitcast(I32)[:, 4 * q:4 * q + 4, :].rearrange("g r m -> r g m"), in_=out_scales[32 * q:32 * q + 4].bitcast(I32))

@@ -34,10 +34,10 @@ FLOPS = 2 * TOKENS * E * F + 2 * TOKENS * F * 2 * BINS
 X_BANKS = (0, 1)
 MM1_BANKS = (2, 3, 4)
 MM2_BANKS = (5, 6)
-U_BANKS = (7, 4, 3, 7)
+U_BANKS = (7, 4, 7, 7)
 DX_BANKS = (0, 1, 2, 3, 4)
 SUM_BANKS = (5, 6)
-SCALAR_SQUARE_EVERY = 8
+SCALAR_SQUARE_EVERY = 10
 
 
 def tile_attractordepthbinhead_x2_kernel(tc, x, w1_words, w1_scales, b1, g, w_head_words, w_head_scales, w_q, out_0, out_1, out_2):
@@ -55,7 +55,9 @@ def tile_attractordepthbinhead_x2_kernel(tc, x, w1_words, w1_scales, b1, g, w_he
         s1_raw = keep.tile([P, PASSES, F], U8, align_bytes=64)
         wh = keep.tile([P, PASSES, 4 * BINS], U8, align_bytes=64)
         sh = keep.tile([P, PASSES, 2 * BINS], U8, align_bytes=64)
+        idle = keep.tile([P, BLOCK], BF16)
         nc.vector.memset(s1_raw[:].bitcast(I32), 0)
+        nc.vector.memset(idle[:], 0.0)
         nc.vector.memset(sh[:].bitcast(I32), 0)
 
         x_raw = {}
@@ -63,17 +65,19 @@ def tile_attractordepthbinhead_x2_kernel(tc, x, w1_words, w1_scales, b1, g, w_he
         def load_x(blk):
             x_raw[blk] = work.tile([P, PACK, E], BF16, tag="x_raw", name="x_raw%d" % blk)
             rows = x[blk * BLOCK:(blk + 1) * BLOCK, :].rearrange("(p t) e -> p t e", t=PACK)
-            for half in range(2):
-                nc.sync.dma_start(out=x_raw[blk][:, 2 * half:2 * half + 2, :], in_=rows[:, 2 * half:2 * half + 2, :])
+            for kp in range(PASSES):
+                nc.sync.dma_start(out=x_raw[blk][:, :, BLOCK * kp:BLOCK * (kp + 1)], in_=rows[:, :, BLOCK * kp:BLOCK * (kp + 1)])
 
         nc.sync.dma_start(out=w1_raw[:].bitcast(I32), in_=w1_words.bitcast(I32).rearrange("g p n -> p g n"))
         load_x(0)
         for q in range(4):
             nc.scalar.dma_start(out=s1_raw[32 * q:32 * q + 4].bitcast(I32), in_=w1_scales.bitcast(I32)[:, 4 * q:4 * q + 4, :].rearrange("g r n -> r g n"))
+        warm = keep.tile([P, 1], F32)
+        nc.scalar.activation(out=warm[:], in_=idle[:, 0:1], func=ACT.Gelu)
         vec = {}
         for name, src in (("b1", b1), ("g", g), ("wq", w_q)):
             vec[name] = keep.tile([P, PASSES, PACK], BF16, name="vec_" + name)
-            nc.scalar.dma_start(out=vec[name][:], in_=src.rearrange("(a p t) -> p a t", a=PASSES, t=PACK))
+            nc.sync.dma_start(out=vec[name][:], in_=src.rearrange("(a p t) -> p a t", a=PASSES, t=PACK))
         load_x(1)
         nc.sync.dma_start(out=wh[:].bitcast(I32), in_=w_head_words.bitcast(I32).rearrange("g p n -> p g n"))
         for q in range(4):
@@ -83,17 +87,16 @@ def tile_attractordepthbinhead_x2_kernel(tc, x, w1_words, w1_scales, b1, g, w_he
         make_identity(nc, ident[:])
         kvec = keep.tile([P, BINS], F32)
         nc.gpsimd.iota(kvec[:], pattern=[[1, BINS]], base=0, channel_multiplier=0, allow_small_or_imprecise_dtypes=True)
+        kcol = keep.tile([P, BINS], F32)
+        nc.gpsimd.iota(kcol[:], pattern=[[0, BINS]], base=0, channel_multiplier=1, allow_small_or_imprecise_dtypes=True)
         lower = keep.tile([P, BINS], F32)
         nc.gpsimd.tensor_scalar(out=lower[:], in0=kvec[:], scalar1=EPS, scalar2=1.0, op0=ALU.add, op1=ALU.mult)
-        bias1 = keep.tile([P, FT], F32)
-        nc.gpsimd.tensor_copy(out=bias1[:], in_=vec["b1"][:].rearrange("p a t -> p (a t)"))
         gw = keep.tile([P, FT], F32)
-        nc.gpsimd.tensor_tensor(out=gw[:], in0=vec["g"][:].rearrange("p a t -> p (a t)"), in1=vec["wq"][:].rearrange("p a t -> p (a t)"), op=ALU.mult)
         half_lc = keep.tile([P, BINS], F32)
-        nc.scalar.activation(out=half_lc[:], in_=lower[:], func=ACT.Ln, scale=1.0 / TRIALS)
-        warm = keep.tile([P, 1], F32)
-        nc.scalar.activation(out=warm[:], in_=lower[:, 0:1], func=ACT.Gelu)
         lc = keep.tile([P, BINS], F32)
+        warm_ps = bank(U_BANKS[0], "warm_ps")
+        for k in range(5):
+            nc.tensor.matmul(out=warm_ps[:], lhsT=idle[:, 0:P], rhs=idle[:], start=True, stop=True)
 
         w1p = keep.tile([P, PASSES, 2 * F], U8, align_bytes=64)
         s1p = keep.tile([P, PASSES, F], U8, align_bytes=64)
@@ -150,52 +153,62 @@ def tile_attractordepthbinhead_x2_kernel(tc, x, w1_words, w1_scales, b1, g, w_he
                                     rhs=xq[blk, kp][:].bitcast(FP8X4), rhs_scale=xs[blk, kp][:], start=(kp == 0), stop=(kp == PASSES - 1))
 
         def gelu(blk, j):
-            nc.scalar.activation(out=gel[:, blk, j, :], in_=z1[blk, j][:], func=ACT.Gelu, bias=bias1[:, j:j + 1])
+            nc.scalar.activation(out=gel[:, blk, j, :], in_=z1[blk, j][:], func=ACT.Gelu, bias=vec["b1"][:, j // PACK, j % PACK:j % PACK + 1])
 
-        def gain_h(blk, a):
-            hg[blk, a] = work.tile([P, BLOCK * PACK], BF16, tag="hg", name="hg%d_%d" % (blk, a), align_bytes=64)
+        def gain_h(blk, a, tps=(0, 1)):
+            if tps[0] == 0:
+                hg[blk, a] = work.tile([P, BLOCK * PACK], BF16, tag="hg", name="hg%d_%d" % (blk, a), align_bytes=64)
+            lo, hi = 2 * P * tps[0], 2 * P * (tps[-1] + 1)
             nc.vector.tensor_tensor(
-                out=hg[blk, a][:].rearrange("p (n t) -> p n t", t=PACK),
-                in0=gel[:, blk, PACK * a:PACK * (a + 1), :].rearrange("p t n -> p n t"),
-                in1=vec["g"][:, a, :].unsqueeze(1).to_broadcast([P, BLOCK, PACK]), op=ALU.mult)
+                out=hg[blk, a][:, PACK * lo:PACK * hi].rearrange("p (n t) -> p n t", t=PACK),
+                in0=gel[:, blk, PACK * a:PACK * (a + 1), lo:hi].rearrange("p t n -> p n t"),
+                in1=vec["g"][:, a, :].unsqueeze(1).to_broadcast([P, hi - lo, PACK]), op=ALU.mult)
 
-        def quant_h(blk, a):
-            hq[blk, a] = work.tile([P, BLOCK], U32, tag="hq", bufs=3, name="hq%d_%d" % (blk, a), align_bytes=64)
-            hs[blk, a] = work.tile([P, BLOCK], U8, tag="hs", bufs=3, name="hs%d_%d" % (blk, a), align_bytes=64)
-            nc.vector.quantize_mx(out=hq[blk, a][:].bitcast(FP8X4), scales=hs[blk, a][:], in_=hg[blk, a][:])
+        def quant_h(blk, a, tps=(0, 1)):
+            if tps[0] == 0:
+                hq[blk, a] = work.tile([P, BLOCK], U32, tag="hq", bufs=3, name="hq%d_%d" % (blk, a), align_bytes=64)
+                hs[blk, a] = work.tile([P, BLOCK], U8, tag="hs", bufs=3, name="hs%d_%d" % (blk, a), align_bytes=64)
+            lo, hi = 2 * P * tps[0], 2 * P * (tps[-1] + 1)
+            nc.vector.quantize_mx(out=hq[blk, a][:, lo:hi].bitcast(FP8X4), scales=hs[blk, a][:, lo:hi], in_=hg[blk, a][:, PACK * lo:PACK * hi])
 
-        def mm2(blk):
-            for tp in range(2):
-                z2[blk, tp] = bank(MM2_BANKS[tp], "z2_%d_%d" % (blk, tp))
-                for t in range(2):
-                    tok = slice(P * (2 * tp + t), P * (2 * tp + t + 1))
-                    for hf in range(2):
-                        col = (2 * t + hf) * BINS
-                        for a in range(PASSES):
-                            nc.tensor.matmul_mx(out=z2[blk, tp][:, col:col + BINS], lhsT=hq[blk, a][:, tok].bitcast(FP8X4), lhsT_scale=hs[blk, a][:, tok],
-                                                rhs=wh[:, a, 2 * BINS * hf:2 * BINS * (hf + 1)].bitcast(FP4X4), rhs_scale=sh[:, a, BINS * hf:BINS * (hf + 1)],
-                                                start=(a == 0), stop=(a == PASSES - 1))
+        def mm2(blk, tp):
+            z2[blk, tp] = bank(MM2_BANKS[tp], "z2_%d_%d" % (blk, tp))
+            for t in range(2):
+                tok = slice(P * (2 * tp + t), P * (2 * tp + t + 1))
+                for hf in range(2):
+                    col = (2 * t + hf) * BINS
+                    for a in range(PASSES):
+                        nc.tensor.matmul_mx(out=z2[blk, tp][:, col:col + BINS], lhsT=hq[blk, a][:, tok].bitcast(FP8X4), lhsT_scale=hs[blk, a][:, tok],
+                                            rhs=wh[:, a, 2 * BINS * hf:2 * BINS * (hf + 1)].bitcast(FP4X4), rhs_scale=sh[:, a, BINS * hf:BINS * (hf + 1)],
+                                            start=(a == 0), stop=(a == PASSES - 1))
 
-        def read_z2(blk, tp):
-            tl = slice(PACK * blk + 2 * tp, PACK * blk + 2 * tp + 2)
-            src = z2[blk, tp][:].rearrange("p (s q i) -> p s i q", q=GROUPS, i=MEMBERS)
-            nc.scalar.activation(out=soft[:, tl].rearrange("p t h (i q) -> p (t h) i q", q=GROUPS), in_=src, func=ACT.Abs)
-            nc.vector.tensor_scalar(out=relu[:, tl].rearrange("p t h (i q) -> p (t h) i q", q=GROUPS), in0=src, scalar1=0.0, scalar2=None, op0=ALU.max)
+        def by_member(tiles):
+            return tiles.rearrange("p t h (i q) -> p (t h) i q", q=GROUPS)
 
-        def soft_block(blk):
-            return soft[:, PACK * blk:PACK * (blk + 1)].rearrange("p t h m -> p (t h m)")
+        def z2_by_member(blk, tp):
+            return z2[blk, tp][:].rearrange("p (s q i) -> p s i q", q=GROUPS, i=MEMBERS)
 
-        def tanh_block(blk):
-            nc.scalar.activation(out=soft_block(blk), in_=soft_block(blk), func=ACT.Tanh, scale=0.5)
+        def abs_z2(blk, tp):
+            first = PACK * blk + 2 * tp
+            nc.scalar.activation(out=by_member(soft[:, first:first + 2]), in_=z2_by_member(blk, tp), func=ACT.Abs)
 
-        def ln_block(blk):
-            nc.scalar.activation(out=soft_block(blk), in_=soft_block(blk), func=ACT.Ln, scale=0.5, bias=0.5)
+        def relu_z2(blk, tp):
+            first = PACK * blk + 2 * tp
+            nc.vector.tensor_scalar(out=by_member(relu[:, first:first + 2]), in0=z2_by_member(blk, tp), scalar1=0.0, scalar2=None, op0=ALU.max)
 
-        def finish_y(blk):
-            tl = slice(PACK * blk, PACK * (blk + 1))
-            nc.vector.scalar_tensor_tensor(out=ytab[:, tl, 0, :], in0=soft[:, tl, 0, :], scalar=BETA, in1=relu[:, tl, 0, :], op0=ALU.add, op1=ALU.subtract)
-            nc.vector.tensor_tensor(out=ytab[:, tl, 1:3, :], in0=relu[:, tl, 1:2, :].to_broadcast([P, PACK, 2, BINS]),
-                                    in1=soft[:, tl, 1:2, :].to_broadcast([P, PACK, 2, BINS]), op=ALU.subtract)
+        def soft_tiles(lo, hi):
+            return soft[:, lo:hi].rearrange("p t h m -> p (t h m)")
+
+        def tanh_tiles(lo, hi):
+            nc.scalar.activation(out=soft_tiles(lo, hi), in_=soft_tiles(lo, hi), func=ACT.Tanh, scale=0.5)
+
+        def ln_tiles(lo, hi):
+            nc.scalar.activation(out=soft_tiles(lo, hi), in_=soft_tiles(lo, hi), func=ACT.Ln, scale=0.5, bias=0.5)
+
+        def finish_y(lo, hi):
+            nc.vector.scalar_tensor_tensor(out=ytab[:, lo:hi, 0, :], in0=soft[:, lo:hi, 0, :], scalar=BETA, in1=relu[:, lo:hi, 0, :], op0=ALU.add, op1=ALU.subtract)
+            nc.vector.tensor_tensor(out=ytab[:, lo:hi, 1:3, :], in0=relu[:, lo:hi, 1:2, :].to_broadcast([P, hi - lo, 2, BINS]),
+                                    in1=soft[:, lo:hi, 1:2, :].to_broadcast([P, hi - lo, 2, BINS]), op=ALU.subtract)
 
         def weigh_u(blk, j):
             nc.vector.tensor_scalar(out=gel[:, blk, j, :], in0=gel[:, blk, j, :], scalar1=gw[:, j:j + 1], scalar2=None, op0=ALU.mult)
@@ -205,12 +218,25 @@ def tile_attractordepthbinhead_x2_kernel(tc, x, w1_words, w1_scales, b1, g, w_he
             if t == 0:
                 u_ps[blk] = bank(U_BANKS[blk], "u_ps%d" % blk)
             for j in range(FT):
-                nc.tensor.matmul(out=u_ps[blk][:, P * t:P * (t + 1)], lhsT=gel[:, blk, j, P * t:P * (t + 1)], rhs=ident[:], start=(j == 0), stop=(j == FT - 1), is_transpose=not (blk in (1, 2) and j % 4 == 0))
+                nc.tensor.matmul(out=u_ps[blk][:, P * t:P * (t + 1)], lhsT=gel[:, blk, j, P * t:P * (t + 1)], rhs=ident[:], start=(j == 0), stop=(j == FT - 1), is_transpose=not (blk == 1 and j % 4 == 0))
 
         def sum_u(blk):
             nc.vector.tensor_reduce(out=u_sum[:, PACK * blk:PACK * (blk + 1)], in_=u_ps[blk][:].rearrange("p (t f) -> p t f", t=PACK), axis=mybir.AxisListType.X, op=ALU.add)
 
-        dx, pair, acc = {}, {}, {}
+        def wide_u(step):
+            duo, j = divmod(step, FT)
+            blk, tp = 2 + duo // 2, duo % 2
+            if j == 0:
+                u_ps[blk, tp] = psum.tile([P, 2 * P], F32, tag="bank%d" % U_BANKS[blk], name="u_wide%d" % duo)
+            nc.tensor.matmul(out=u_ps[blk, tp][:], lhsT=gw[:, j:j + 1].to_broadcast([P, P]), rhs=gel[:, blk, j, 2 * P * tp:2 * P * (tp + 1)], start=(j == 0), stop=(j == FT - 1))
+            if j == FT - 1:
+                for t in range(2):
+                    tile = PACK * blk + 2 * tp + t
+                    masked = work.tile([P, P], F32, tag="masked", name="masked%d" % tile)
+                    nc.vector.scalar_tensor_tensor(out=masked[:], in0=u_ps[blk, tp][:, P * t:P * (t + 1)], scalar=1.0, in1=ident[:], op0=ALU.mult, op1=ALU.mult,
+                                                   accum_out=u_sum[:, tile:tile + 1])
+
+        dx, pair, fold, acc = {}, {}, {}, {}
 
         def make_dx(n, k):
             tile, part = divmod(n, MEMBERS // SHIFTS)
@@ -218,12 +244,12 @@ def tile_attractordepthbinhead_x2_kernel(tc, x, w1_words, w1_scales, b1, g, w_he
                 dx[n] = bank(DX_BANKS[n % len(DX_BANKS)], "dx%d" % n)
             row = ytab[:, tile].rearrange("p s m -> p (s m)")
             start = BINS + GROUPS * (SHIFTS * part + k)
-            plain = k in ((0, 2) if n < 6 else (0, 3) if n % 2 == 0 else (1,))
+            plain = n >= 48 and k in ((0, 3), (2,), (1,), (0,))[n % 4]
             nc.tensor.matmul(out=dx[n][:, P * k:P * (k + 1)], lhsT=row[:, start:start + BINS], rhs=ident[:], start=True, stop=False, is_transpose=True)
             nc.tensor.matmul(out=dx[n][:, P * k:P * (k + 1)], lhsT=row[:, 0:BINS], rhs=ident[:], start=False, stop=True, is_transpose=not plain)
 
         def square_dx(n):
-            pair[n] = work.tile([P, BLOCK], F32, tag="pair", bufs=7, name="pair%d" % n)
+            pair[n] = work.tile([P, BLOCK], F32, tag="pair", bufs=8, name="pair%d" % n)
             nc.scalar.activation(out=pair[n][:], in_=dx[n][:], func=ACT.Square, bias=-BETA)
 
         def rsqrt(n):
@@ -233,17 +259,28 @@ def tile_attractordepthbinhead_x2_kernel(tc, x, w1_words, w1_scales, b1, g, w_he
             nc.vector.tensor_tensor(out=pair[n][:], in0=dx[n][:], in1=pair[n][:], op=ALU.mult)
 
         def square_e(n):
-            if n % SCALAR_SQUARE_EVERY == 3:
+            if n % SCALAR_SQUARE_EVERY == 0:
                 nc.scalar.activation(out=pair[n][:], in_=pair[n][:], func=ACT.Square)
             else:
-                nc.vector.tensor_tensor(out=pair[n][:], in0=pair[n][:], in1=pair[n][:], op=ALU.mult)
+                nc.gpsimd.tensor_tensor(out=pair[n][:], in0=pair[n][:], in1=pair[n][:], op=ALU.mult)
+
+        def folded(n):
+            return n % 8 in (0, 1, 2, 4, 6)
+
+        def fold_e(n):
+            if folded(n):
+                fold[n] = work.tile([P, P], F32, tag="fold", bufs=3, name="fold%d" % n)
+                nc.vector.tensor_reduce(out=fold[n][:], in_=pair[n][:].rearrange("p (s r) -> p r s", s=SHIFTS), axis=mybir.AxisListType.X, op=ALU.add)
 
         def reduce_e(n, k):
             tile, part = divmod(n, MEMBERS // SHIFTS)
+            if folded(n) and k > 0:
+                return
             s = SHIFTS * part + k
             if s == 0:
                 acc[tile] = psum.tile([P, BINS], F32, tag="bank%d" % SUM_BANKS[tile % 2], name="acc%d" % tile)
-            nc.tensor.matmul(out=acc[tile][:], lhsT=pair[n][:, P * k:P * (k + 1)], rhs=ident[:], start=(s == 0), stop=(s == MEMBERS - 1), is_transpose=True)
+            src = fold[n][:] if folded(n) else pair[n][:, P * k:P * (k + 1)]
+            nc.tensor.matmul(out=acc[tile][:], lhsT=src, rhs=ident[:], start=(s == 0), stop=(s == MEMBERS - 1), is_transpose=True)
 
         def centres(tile):
             nc.vector.scalar_tensor_tensor(out=res[:, tile, :].rearrange("p (q i) -> p q i", i=MEMBERS), in0=acc[tile][:].rearrange("p (i q) -> p q i", q=GROUPS),
@@ -254,7 +291,7 @@ def tile_attractordepthbinhead_x2_kernel(tc, x, w1_words, w1_scales, b1, g, w_he
             nc.vector.tensor_scalar(out=shift[:], in0=u_sum[:], scalar1=0.0, scalar2=-TRIALS / TEMP, op0=ALU.max, op1=ALU.mult)
 
         def make_logits(tile):
-            nc.vector.scalar_tensor_tensor(out=logit[:, tile, :], in0=kvec[:], scalar=slope[:, tile:tile + 1], in1=lc[:], op0=ALU.mult, op1=ALU.add)
+            nc.vector.scalar_tensor_tensor(out=logit[:, tile, :], in0=k_ps[:], scalar=slope[:, tile:tile + 1], in1=lc[:], op0=ALU.mult, op1=ALU.add)
 
         def exp_tile(tile):
             nc.scalar.activation(out=logit[:, tile, :], in_=logit[:, tile, :], func=ACT.Exp, bias=shift[:, tile:tile + 1], accum_out=total[:, tile:tile + 1])
@@ -268,10 +305,9 @@ def tile_attractordepthbinhead_x2_kernel(tc, x, w1_words, w1_scales, b1, g, w_he
             if b % 2 == 1:
                 quant_x(0, b // 2)
         permute_w1(1)
-        nc.vector.scalar_tensor_tensor(out=half_lc[:], in0=lower[:], scalar=-1.0 / TEMP, in1=half_lc[:], op0=ALU.mult, op1=ALU.mult)
+        nc.vector.tensor_tensor(out=gw[:], in0=vec["g"][:].rearrange("p a t -> p (a t)"), in1=vec["wq"][:].rearrange("p a t -> p (a t)"), op=ALU.mult)
         for j in range(3):
             mm1(0, j)
-        nc.vector.tensor_tensor(out=lc[:], in0=half_lc[:], in1=half_lc[:, ::-1], op=ALU.add)
         for blk in range(BLOCKS):
             more, prev = blk + 1 < BLOCKS, blk > 0
             if prev:
@@ -299,7 +335,8 @@ def tile_attractordepthbinhead_x2_kernel(tc, x, w1_words, w1_scales, b1, g, w_he
             gelu(blk, 3)
             gain_h(blk, 0)
             if prev:
-                mm2(blk - 1)
+                mm2(blk - 1, 0)
+                mm2(blk - 1, 1)
             mm1(blk, 6)
             if more:
                 copy_x(blk + 1, 2)
@@ -309,51 +346,61 @@ def tile_attractordepthbinhead_x2_kernel(tc, x, w1_words, w1_scales, b1, g, w_he
             gelu(blk, 4)
             mm1(blk, 7)
             if prev:
-                read_z2(blk - 1, 0)
-                read_z2(blk - 1, 1)
+                for tp in range(2):
+                    if more:
+                        abs_z2(blk - 1, tp)
+                    relu_z2(blk - 1, tp)
             for j in range(PACK):
                 weigh_u(blk // 2, PACK * (blk % 2) + j)
             for j in range(5, 8):
                 gelu(blk, j)
                 if more:
                     mm1(blk + 1, j - 5)
-            if prev:
-                tanh_block(blk - 1)
+            if prev and more:
+                tanh_tiles(PACK * (blk - 1), PACK * blk)
         last = BLOCKS - 1
-        gain_h(last, 1)
-        for tile in range(PACK):
+        gain_h(last, 1, (0,))
+        abs_z2(last - 1, 0)
+        abs_z2(last - 1, 1)
+        tanh_tiles(PACK * (last - 1), PACK * last)
+        for tile in range(2):
             turn_u(tile)
-        weigh_u(2, 0)
-        quant_h(last, 1)
-        mm2(last)
-        for j in range(1, 4):
-            weigh_u(2, j)
-        read_z2(last, 0)
-        read_z2(last, 1)
-        tanh_block(last)
-        for tile in range(PACK, 2 * PACK):
+        gain_h(last, 1, (1,))
+        for tp in range(2):
+            quant_h(last, 1, (tp,))
+            mm2(last, tp)
+        for tp in range(2):
+            abs_z2(last, tp)
+            relu_z2(last, tp)
+        tanh_tiles(PACK * last, PACK * last + 2)
+        tanh_tiles(PACK * last + 2, TILES)
+        for tile in range(2, 2 * PACK):
             turn_u(tile)
-        for j in range(PACK, FT):
-            weigh_u(2, j)
-        for tile in range(2 * PACK, 3 * PACK):
-            turn_u(tile)
-        sum_u(0)
-        sum_u(1)
-        for blk in range(BLOCKS):
-            ln_block(blk)
-            finish_y(blk)
-            if blk == 0:
-                sum_u(2)
-
+        ln_tiles(0, 1)
+        finish_y(0, 1)
         for k in range(SHIFTS):
             make_dx(0, k)
+        ln_tiles(1, PACK)
+        sum_u(1)
+        finish_y(1, PACK)
+        sum_u(0)
+        for blk in range(1, BLOCKS):
+            ln_tiles(PACK * blk, PACK * (blk + 1))
+        nc.scalar.activation(out=half_lc[:], in_=lower[:], func=ACT.Ln, scale=1.0 / TRIALS)
+
         logits_next = 0
-        for k in range(CHUNKS + 6):
+        for blk in range(1, BLOCKS):
+            finish_y(PACK * blk, PACK * (blk + 1))
+        nc.vector.scalar_tensor_tensor(out=half_lc[:], in0=lower[:], scalar=-1.0 / TEMP, in1=half_lc[:], op0=ALU.mult, op1=ALU.mult)
+        nc.vector.tensor_tensor(out=lc[:], in0=half_lc[:], in1=half_lc[:, ::-1], op=ALU.add)
+        for k in range(CHUNKS + 7):
             for c in range(SHIFTS):
                 if k + 1 < CHUNKS:
                     make_dx(k + 1, c)
-                if 0 <= k - 5 < CHUNKS:
-                    reduce_e(k - 5, c)
+                if 0 <= k - 6 < CHUNKS:
+                    reduce_e(k - 6, c)
+                if (SHIFTS * k + c) % 6 == 0 and (SHIFTS * k + c) // 6 < 4 * FT:
+                    wide_u((SHIFTS * k + c) // 6)
             if k < CHUNKS:
                 square_dx(k)
             if 0 <= k - 1 < CHUNKS:
@@ -362,17 +409,15 @@ def tile_attractordepthbinhead_x2_kernel(tc, x, w1_words, w1_scales, b1, g, w_he
                 weigh(k - 2)
             if 0 <= k - 3 < CHUNKS:
                 square_e(k - 3)
-            if k >= 6 and (k - 6) % 4 == 3:
-                centres((k - 6) // 4)
-            if k % 2 == 0 and k < 16:
-                weigh_u(last, k // 2)
-            if k % 4 == 0 and 16 <= k < 32:
-                turn_u(3 * PACK + (k - 16) // 4)
-            if k == 33:
-                sum_u(last)
-            if k == 40:
+            if 0 <= k - 4 < CHUNKS:
+                fold_e(k - 4)
+            if k >= 7 and (k - 7) % 4 == 3:
+                centres((k - 7) // 4)
+            if k == 48:
+                k_ps = psum.tile([P, BINS], F32, tag="bank%d" % U_BANKS[last], name="k_ps")
+                nc.tensor.transpose(k_ps[:], kcol[:], ident[:])
                 slopes()
-            if k > 41 and logits_next < TILES:
+            if k > 49 and logits_next < TILES:
                 make_logits(logits_next)
                 logits_next += 1
 

@@ -22,22 +22,36 @@ BLOCK = P * PACK
 BLOCKS = TOKENS // BLOCK
 TILES = TOKENS // P
 PASSES = E // BLOCK
-FT = F // P
+FEATURE_TILES = F // P
+QUADRANTS = 4
 SHIFTS = 4
-CHUNKS = TILES * MEMBERS // SHIFTS
+PARTS = MEMBERS // SHIFTS
+CHUNKS = TILES * PARTS
 BETA = 1.0 / math.sqrt(2.0)
 EPS = 1e-6
-TEMP = 20.0
+TEMPERATURE = 20.0
 TRIALS = BINS - 1
 FLOPS = 2 * TOKENS * E * F + 2 * TOKENS * F * 2 * BINS
 
 X_BANKS = (0, 1)
 MM1_BANKS = (2, 3, 4)
 MM2_BANKS = (5, 6)
-U_BANKS = (7, 4, 7, 7)
-DX_BANKS = (0, 1, 2, 3, 4)
+U_BANK = 7
+D_BANKS = (0, 1, 2, 3, 4)
 SUM_BANKS = (5, 6)
-SCALAR_SQUARE_EVERY = 10
+FIRST_WIDE_BANK = D_BANKS[-1]
+
+WARM_UP_MATMULS = 5
+SCALAR_SQUARE_EVERY = 4
+RSQRT_LAG, WEIGH_LAG, SQUARE_LAG, REDUCE_LAG, CENTRE_LAG = 1, 2, 3, 6, 7
+
+DUOS = 2 * (BLOCKS - 1)
+WOVEN = (DUOS - 1) * FEATURE_TILES
+EARLY_WIDE_AT = [0, 5, 10, 15, 15, 15, 15]
+WIDE_AT = EARLY_WIDE_AT + [21 + 13 * s // 2 for s in range(WOVEN - len(EARLY_WIDE_AT))]
+PLAIN_FROM_CHUNK = 60
+PLAIN_SHIFTS = ((0, 3), (2,), (1,), (0,))
+SLOPES_STEP, LAST_SLOPES_STEP, FIRST_LOGITS_STEP = 48, 60, 50
 
 
 def tile_attractordepthbinhead_x2_kernel(tc, x, w1_words, w1_scales, b1, g, w_head_words, w_head_scales, w_q, out_0, out_1, out_2):
@@ -48,16 +62,16 @@ def tile_attractordepthbinhead_x2_kernel(tc, x, w1_words, w1_scales, b1, g, w_he
         psum = ctx.enter_context(tc.psum_pool(name="psum", bufs=1))
         ctx.enter_context(tc.manual_schedule())
 
-        def bank(b, name):
-            return psum.tile([P, BLOCK], F32, tag="bank%d" % b, name=name)
+        def bank(b, name, width=BLOCK):
+            return psum.tile([P, width], F32, tag="bank%d" % b, name=name)
 
         w1_raw = keep.tile([P, PASSES, 2 * F], U8, align_bytes=64)
         s1_raw = keep.tile([P, PASSES, F], U8, align_bytes=64)
         wh = keep.tile([P, PASSES, 4 * BINS], U8, align_bytes=64)
         sh = keep.tile([P, PASSES, 2 * BINS], U8, align_bytes=64)
-        idle = keep.tile([P, BLOCK], BF16)
+        zeros = keep.tile([P, BLOCK], BF16)
         nc.vector.memset(s1_raw[:].bitcast(I32), 0)
-        nc.vector.memset(idle[:], 0.0)
+        nc.vector.memset(zeros[:], 0.0)
         nc.vector.memset(sh[:].bitcast(I32), 0)
 
         x_raw = {}
@@ -68,35 +82,35 @@ def tile_attractordepthbinhead_x2_kernel(tc, x, w1_words, w1_scales, b1, g, w_he
             for kp in range(PASSES):
                 nc.sync.dma_start(out=x_raw[blk][:, :, BLOCK * kp:BLOCK * (kp + 1)], in_=rows[:, :, BLOCK * kp:BLOCK * (kp + 1)])
 
+        def load_scales(queue, plane, rows):
+            for q in range(QUADRANTS):
+                queue.dma_start(out=plane[32 * q:32 * q + 4].bitcast(I32), in_=rows.bitcast(I32)[:, 4 * q:4 * q + 4, :].rearrange("g r n -> r g n"))
+
         nc.sync.dma_start(out=w1_raw[:].bitcast(I32), in_=w1_words.bitcast(I32).rearrange("g p n -> p g n"))
         load_x(0)
-        for q in range(4):
-            nc.scalar.dma_start(out=s1_raw[32 * q:32 * q + 4].bitcast(I32), in_=w1_scales.bitcast(I32)[:, 4 * q:4 * q + 4, :].rearrange("g r n -> r g n"))
+        load_scales(nc.scalar, s1_raw, w1_scales)
         warm = keep.tile([P, 1], F32)
-        nc.scalar.activation(out=warm[:], in_=idle[:, 0:1], func=ACT.Gelu)
+        nc.scalar.activation(out=warm[:], in_=zeros[:, 0:1], func=ACT.Gelu)
         vec = {}
         for name, src in (("b1", b1), ("g", g), ("wq", w_q)):
             vec[name] = keep.tile([P, PASSES, PACK], BF16, name="vec_" + name)
             nc.sync.dma_start(out=vec[name][:], in_=src.rearrange("(a p t) -> p a t", a=PASSES, t=PACK))
         load_x(1)
         nc.sync.dma_start(out=wh[:].bitcast(I32), in_=w_head_words.bitcast(I32).rearrange("g p n -> p g n"))
-        for q in range(4):
-            nc.sync.dma_start(out=sh[32 * q:32 * q + 4].bitcast(I32), in_=w_head_scales.bitcast(I32)[:, 4 * q:4 * q + 4, :].rearrange("g r n -> r g n"))
+        load_scales(nc.sync, sh, w_head_scales)
 
         ident = keep.tile([P, P], F32)
         make_identity(nc, ident[:])
         kvec = keep.tile([P, BINS], F32)
         nc.gpsimd.iota(kvec[:], pattern=[[1, BINS]], base=0, channel_multiplier=0, allow_small_or_imprecise_dtypes=True)
-        kcol = keep.tile([P, BINS], F32)
-        nc.gpsimd.iota(kcol[:], pattern=[[0, BINS]], base=0, channel_multiplier=1, allow_small_or_imprecise_dtypes=True)
         lower = keep.tile([P, BINS], F32)
         nc.gpsimd.tensor_scalar(out=lower[:], in0=kvec[:], scalar1=EPS, scalar2=1.0, op0=ALU.add, op1=ALU.mult)
-        gw = keep.tile([P, FT], F32)
+        gw = keep.tile([P, FEATURE_TILES], F32)
         half_lc = keep.tile([P, BINS], F32)
         lc = keep.tile([P, BINS], F32)
-        warm_ps = bank(U_BANKS[0], "warm_ps")
-        for k in range(5):
-            nc.tensor.matmul(out=warm_ps[:], lhsT=idle[:, 0:P], rhs=idle[:], start=True, stop=True)
+        warm_ps = bank(U_BANK, "warm_ps")
+        for k in range(WARM_UP_MATMULS):
+            nc.tensor.matmul(out=warm_ps[:], lhsT=zeros[:, 0:P], rhs=zeros[:], start=True, stop=True)
 
         w1p = keep.tile([P, PASSES, 2 * F], U8, align_bytes=64)
         s1p = keep.tile([P, PASSES, F], U8, align_bytes=64)
@@ -110,7 +124,7 @@ def tile_attractordepthbinhead_x2_kernel(tc, x, w1_words, w1_scales, b1, g, w_he
                 out=s1p[:, :, BLOCK * a:BLOCK * (a + 1)].rearrange("p g (t m) -> p g t m", t=PACK),
                 in_=s1_raw[:, :, BLOCK * a:BLOCK * (a + 1)].rearrange("p g (m t) -> p g t m", t=PACK))
 
-        gel = keep.tile([P, BLOCKS, FT, BLOCK], F32)
+        gel = keep.tile([P, BLOCKS, FEATURE_TILES, BLOCK], F32)
         soft = keep.tile([P, TILES, 2, BINS], F32)
         relu = keep.tile([P, TILES, 2, BINS], F32)
         ytab = keep.tile([P, TILES, 3, BINS], F32)
@@ -122,8 +136,7 @@ def tile_attractordepthbinhead_x2_kernel(tc, x, w1_words, w1_scales, b1, g, w_he
         norm = keep.tile([P, TILES], F32)
         out_scales = keep.tile([P, BLOCKS, BINS], U8, align_bytes=64)
         u_sum = keep.tile([P, TILES], F32)
-        u_ps = {}
-        xt, xg, xq, xs, z1, hg, hq, hs, z2 = {}, {}, {}, {}, {}, {}, {}, {}, {}
+        xt, xg, xq, xs, z1, hg, hq, hs, z2, u_wide = {}, {}, {}, {}, {}, {}, {}, {}, {}, {}
 
         def turn_x(blk, b, banks=X_BANKS):
             kp, tp = divmod(b, 2)
@@ -142,12 +155,12 @@ def tile_attractordepthbinhead_x2_kernel(tc, x, w1_words, w1_scales, b1, g, w_he
             nc.scalar.copy(out=dst.rearrange("p (t r u) -> p t r u", t=2, u=2), in_=xt[blk, b][:].rearrange("p (t u r) -> p t r u", t=2, u=2))
 
         def quant_x(blk, kp):
-            xq[blk, kp] = work.tile([P, BLOCK], U32, tag="xq", bufs=4, name="xq%d_%d" % (blk, kp), align_bytes=64)
-            xs[blk, kp] = work.tile([P, BLOCK], U8, tag="xs", bufs=4, name="xs%d_%d" % (blk, kp), align_bytes=64)
+            xq[blk, kp] = work.tile([P, BLOCK], U32, tag="xq", bufs=2 * PASSES, name="xq%d_%d" % (blk, kp), align_bytes=64)
+            xs[blk, kp] = work.tile([P, BLOCK], U8, tag="xs", bufs=2 * PASSES, name="xs%d_%d" % (blk, kp), align_bytes=64)
             nc.vector.quantize_mx(out=xq[blk, kp][:].bitcast(FP8X4), scales=xs[blk, kp][:], in_=xg[blk, kp][:])
 
         def mm1(blk, j):
-            z1[blk, j] = bank(MM1_BANKS[(FT * blk + j) % len(MM1_BANKS)], "z1_%d_%d" % (blk, j))
+            z1[blk, j] = bank(MM1_BANKS[(FEATURE_TILES * blk + j) % len(MM1_BANKS)], "z1_%d_%d" % (blk, j))
             for kp in range(PASSES):
                 nc.tensor.matmul_mx(out=z1[blk, j][:], lhsT=w1p[:, kp, 2 * P * j:2 * P * (j + 1)].bitcast(FP4X4), lhsT_scale=s1p[:, kp, P * j:P * (j + 1)],
                                     rhs=xq[blk, kp][:].bitcast(FP8X4), rhs_scale=xs[blk, kp][:], start=(kp == 0), stop=(kp == PASSES - 1))
@@ -166,8 +179,8 @@ def tile_attractordepthbinhead_x2_kernel(tc, x, w1_words, w1_scales, b1, g, w_he
 
         def quant_h(blk, a, tps=(0, 1)):
             if tps[0] == 0:
-                hq[blk, a] = work.tile([P, BLOCK], U32, tag="hq", bufs=3, name="hq%d_%d" % (blk, a), align_bytes=64)
-                hs[blk, a] = work.tile([P, BLOCK], U8, tag="hs", bufs=3, name="hs%d_%d" % (blk, a), align_bytes=64)
+                hq[blk, a] = work.tile([P, BLOCK], U32, tag="hq", bufs=PASSES + 1, name="hq%d_%d" % (blk, a), align_bytes=64)
+                hs[blk, a] = work.tile([P, BLOCK], U8, tag="hs", bufs=PASSES + 1, name="hs%d_%d" % (blk, a), align_bytes=64)
             lo, hi = 2 * P * tps[0], 2 * P * (tps[-1] + 1)
             nc.vector.quantize_mx(out=hq[blk, a][:, lo:hi].bitcast(FP8X4), scales=hs[blk, a][:, lo:hi], in_=hg[blk, a][:, PACK * lo:PACK * hi])
 
@@ -210,115 +223,107 @@ def tile_attractordepthbinhead_x2_kernel(tc, x, w1_words, w1_scales, b1, g, w_he
             nc.vector.tensor_tensor(out=ytab[:, lo:hi, 1:3, :], in0=relu[:, lo:hi, 1:2, :].to_broadcast([P, hi - lo, 2, BINS]),
                                     in1=soft[:, lo:hi, 1:2, :].to_broadcast([P, hi - lo, 2, BINS]), op=ALU.subtract)
 
-        def weigh_u(blk, j):
-            nc.vector.tensor_scalar(out=gel[:, blk, j, :], in0=gel[:, blk, j, :], scalar1=gw[:, j:j + 1], scalar2=None, op0=ALU.mult)
+        def weigh_u0(j):
+            nc.vector.tensor_scalar(out=gel[:, 0, j, :], in0=gel[:, 0, j, :], scalar1=gw[:, j:j + 1], scalar2=None, op0=ALU.mult)
 
-        def turn_u(tile):
-            blk, t = divmod(tile, PACK)
-            if t == 0:
-                u_ps[blk] = bank(U_BANKS[blk], "u_ps%d" % blk)
-            for j in range(FT):
-                nc.tensor.matmul(out=u_ps[blk][:, P * t:P * (t + 1)], lhsT=gel[:, blk, j, P * t:P * (t + 1)], rhs=ident[:], start=(j == 0), stop=(j == FT - 1), is_transpose=not (blk == 1 and j % 4 == 0))
+        def turn_u0(u0_ps, t):
+            for j in range(FEATURE_TILES):
+                nc.tensor.matmul(out=u0_ps[:, P * t:P * (t + 1)], lhsT=gel[:, 0, j, P * t:P * (t + 1)], rhs=ident[:],
+                                 start=(j == 0), stop=(j == FEATURE_TILES - 1), is_transpose=True)
 
-        def sum_u(blk):
-            nc.vector.tensor_reduce(out=u_sum[:, PACK * blk:PACK * (blk + 1)], in_=u_ps[blk][:].rearrange("p (t f) -> p t f", t=PACK), axis=mybir.AxisListType.X, op=ALU.add)
-
-        def wide_u(step):
-            duo, j = divmod(step, FT)
-            blk, tp = 2 + duo // 2, duo % 2
+        def wide_u(index):
+            duo, j = divmod(index, FEATURE_TILES)
+            blk, tp = 1 + duo // 2, duo % 2
             if j == 0:
-                u_ps[blk, tp] = psum.tile([P, 2 * P], F32, tag="bank%d" % U_BANKS[blk], name="u_wide%d" % duo)
-            nc.tensor.matmul(out=u_ps[blk, tp][:], lhsT=gw[:, j:j + 1].to_broadcast([P, P]), rhs=gel[:, blk, j, 2 * P * tp:2 * P * (tp + 1)], start=(j == 0), stop=(j == FT - 1))
-            if j == FT - 1:
-                for t in range(2):
-                    tile = PACK * blk + 2 * tp + t
-                    masked = work.tile([P, P], F32, tag="masked", name="masked%d" % tile)
-                    nc.vector.scalar_tensor_tensor(out=masked[:], in0=u_ps[blk, tp][:, P * t:P * (t + 1)], scalar=1.0, in1=ident[:], op0=ALU.mult, op1=ALU.mult,
-                                                   accum_out=u_sum[:, tile:tile + 1])
+                u_wide[duo] = bank(FIRST_WIDE_BANK if duo == 0 else U_BANK, "u_wide%d" % duo, 2 * P)
+            nc.tensor.matmul(out=u_wide[duo][:], lhsT=gw[:, j:j + 1].to_broadcast([P, P]), rhs=gel[:, blk, j, 2 * P * tp:2 * P * (tp + 1)],
+                             start=(j == 0), stop=(j == FEATURE_TILES - 1))
 
-        dx, pair, fold, acc = {}, {}, {}, {}
+        def pick_u(duo):
+            for t in range(2):
+                tile = PACK + 2 * duo + t
+                masked = work.tile([P, P], F32, tag="masked", name="masked%d" % tile)
+                nc.vector.scalar_tensor_tensor(out=masked[:], in0=u_wide[duo][:, P * t:P * (t + 1)], scalar=1.0, in1=ident[:], op0=ALU.mult, op1=ALU.mult,
+                                               accum_out=u_sum[:, tile:tile + 1])
 
-        def make_dx(n, k):
-            tile, part = divmod(n, MEMBERS // SHIFTS)
+        d_ps, chunk, chunk_pair, acc = {}, {}, {}, {}
+
+        def make_d(n, k):
+            tile, part = divmod(n, PARTS)
             if k == 0:
-                dx[n] = bank(DX_BANKS[n % len(DX_BANKS)], "dx%d" % n)
+                d_ps[n] = bank(D_BANKS[n % len(D_BANKS)], "d%d" % n)
             row = ytab[:, tile].rearrange("p s m -> p (s m)")
             start = BINS + GROUPS * (SHIFTS * part + k)
-            plain = n >= 48 and k in ((0, 3), (2,), (1,), (0,))[n % 4]
-            nc.tensor.matmul(out=dx[n][:, P * k:P * (k + 1)], lhsT=row[:, start:start + BINS], rhs=ident[:], start=True, stop=False, is_transpose=True)
-            nc.tensor.matmul(out=dx[n][:, P * k:P * (k + 1)], lhsT=row[:, 0:BINS], rhs=ident[:], start=False, stop=True, is_transpose=not plain)
+            plain = n >= PLAIN_FROM_CHUNK and k in PLAIN_SHIFTS[n % len(PLAIN_SHIFTS)]
+            nc.tensor.matmul(out=d_ps[n][:, P * k:P * (k + 1)], lhsT=row[:, start:start + BINS], rhs=ident[:], start=True, stop=False, is_transpose=True)
+            nc.tensor.matmul(out=d_ps[n][:, P * k:P * (k + 1)], lhsT=row[:, 0:BINS], rhs=ident[:], start=False, stop=True, is_transpose=not plain)
 
         def square_dx(n):
-            pair[n] = work.tile([P, BLOCK], F32, tag="pair", bufs=8, name="pair%d" % n)
-            nc.scalar.activation(out=pair[n][:], in_=dx[n][:], func=ACT.Square, bias=-BETA)
+            if n % 2 == 0:
+                chunk_pair[n // 2] = work.tile([P, 2, BLOCK], F32, tag="pair", bufs=5, name="pair%d" % n)
+            chunk[n] = chunk_pair[n // 2][:, n % 2, :]
+            nc.scalar.activation(out=chunk[n], in_=d_ps[n][:], func=ACT.Square, bias=-BETA)
 
         def rsqrt(n):
-            nc.scalar.activation(out=pair[n][:], in_=pair[n][:], func=ACT.Abs_reciprocal_sqrt, scale=2.0, bias=1.0)
+            nc.scalar.activation(out=chunk[n], in_=chunk[n], func=ACT.Abs_reciprocal_sqrt, scale=2.0, bias=1.0)
 
         def weigh(n):
-            nc.vector.tensor_tensor(out=pair[n][:], in0=dx[n][:], in1=pair[n][:], op=ALU.mult)
+            nc.vector.tensor_tensor(out=chunk[n], in0=d_ps[n][:], in1=chunk[n], op=ALU.mult)
 
         def square_e(n):
-            if n % SCALAR_SQUARE_EVERY == 0:
-                nc.scalar.activation(out=pair[n][:], in_=pair[n][:], func=ACT.Square)
+            shared = (n // 2) % SCALAR_SQUARE_EVERY == 1
+            if n % 2 == 0:
+                if shared:
+                    nc.scalar.activation(out=chunk[n], in_=chunk[n], func=ACT.Square)
             else:
-                nc.gpsimd.tensor_tensor(out=pair[n][:], in0=pair[n][:], in1=pair[n][:], op=ALU.mult)
-
-        def folded(n):
-            return n % 8 in (0, 1, 2, 4, 6)
-
-        def fold_e(n):
-            if folded(n):
-                fold[n] = work.tile([P, P], F32, tag="fold", bufs=3, name="fold%d" % n)
-                nc.vector.tensor_reduce(out=fold[n][:], in_=pair[n][:].rearrange("p (s r) -> p r s", s=SHIFTS), axis=mybir.AxisListType.X, op=ALU.add)
+                span = chunk[n] if shared else chunk_pair[n // 2][:].rearrange("p d c -> p (d c)")
+                nc.vector.tensor_tensor(out=span, in0=span, in1=span, op=ALU.mult)
 
         def reduce_e(n, k):
-            tile, part = divmod(n, MEMBERS // SHIFTS)
-            if folded(n) and k > 0:
-                return
+            tile, part = divmod(n, PARTS)
             s = SHIFTS * part + k
             if s == 0:
-                acc[tile] = psum.tile([P, BINS], F32, tag="bank%d" % SUM_BANKS[tile % 2], name="acc%d" % tile)
-            src = fold[n][:] if folded(n) else pair[n][:, P * k:P * (k + 1)]
-            nc.tensor.matmul(out=acc[tile][:], lhsT=src, rhs=ident[:], start=(s == 0), stop=(s == MEMBERS - 1), is_transpose=True)
+                acc[tile] = bank(SUM_BANKS[tile % 2], "acc%d" % tile, BINS)
+            nc.tensor.matmul(out=acc[tile][:], lhsT=chunk[n][:, P * k:P * (k + 1)], rhs=ident[:], start=(s == 0), stop=(s == MEMBERS - 1), is_transpose=True)
 
         def centres(tile):
             nc.vector.scalar_tensor_tensor(out=res[:, tile, :].rearrange("p (q i) -> p q i", i=MEMBERS), in0=acc[tile][:].rearrange("p (i q) -> p q i", q=GROUPS),
                                            scalar=2.0 * BETA / MEMBERS, in1=ytab[:, tile, 0, :].rearrange("p (i q) -> p q i", q=GROUPS), op0=ALU.mult, op1=ALU.subtract)
 
-        def slopes():
-            nc.vector.tensor_scalar(out=slope[:], in0=u_sum[:], scalar1=1.0 / TEMP, scalar2=None, op0=ALU.mult)
-            nc.vector.tensor_scalar(out=shift[:], in0=u_sum[:], scalar1=0.0, scalar2=-TRIALS / TEMP, op0=ALU.max, op1=ALU.mult)
+        def slopes(lo, hi):
+            nc.vector.tensor_scalar(out=slope[:, lo:hi], in0=u_sum[:, lo:hi], scalar1=1.0 / TEMPERATURE, scalar2=None, op0=ALU.mult)
+            nc.vector.tensor_scalar(out=shift[:, lo:hi], in0=slope[:, lo:hi], scalar1=0.0, scalar2=-float(TRIALS), op0=ALU.max, op1=ALU.mult)
 
         def make_logits(tile):
-            nc.vector.scalar_tensor_tensor(out=logit[:, tile, :], in0=k_ps[:], scalar=slope[:, tile:tile + 1], in1=lc[:], op0=ALU.mult, op1=ALU.add)
+            nc.vector.scalar_tensor_tensor(out=logit[:, tile, :], in0=kvec[:], scalar=slope[:, tile:tile + 1], in1=lc[:], op0=ALU.mult, op1=ALU.add)
 
         def exp_tile(tile):
             nc.scalar.activation(out=logit[:, tile, :], in_=logit[:, tile, :], func=ACT.Exp, bias=shift[:, tile:tile + 1], accum_out=total[:, tile:tile + 1])
 
+        ahead = len(MM1_BANKS)
+        last = BLOCKS - 1
         permute_w1(0)
-        for b in range(4):
+        for b in range(2 * PASSES):
             turn_x(0, b, X_BANKS + MM2_BANKS)
         load_x(2)
-        for b in range(4):
+        for b in range(2 * PASSES):
             copy_x(0, b)
             if b % 2 == 1:
                 quant_x(0, b // 2)
         permute_w1(1)
         nc.vector.tensor_tensor(out=gw[:], in0=vec["g"][:].rearrange("p a t -> p (a t)"), in1=vec["wq"][:].rearrange("p a t -> p (a t)"), op=ALU.mult)
-        for j in range(3):
+        for j in range(ahead):
             mm1(0, j)
         for blk in range(BLOCKS):
-            more, prev = blk + 1 < BLOCKS, blk > 0
+            more, prev = blk < last, blk > 0
             if prev:
                 gain_h(blk - 1, 1)
             if more:
                 turn_x(blk + 1, 0)
                 turn_x(blk + 1, 1)
-            gelu(blk, 0)
-            mm1(blk, 3)
-            gelu(blk, 1)
-            mm1(blk, 4)
+            for j in (0, 1):
+                gelu(blk, j)
+                mm1(blk, j + ahead)
             if more:
                 copy_x(blk + 1, 0)
                 copy_x(blk + 1, 1)
@@ -331,40 +336,41 @@ def tile_attractordepthbinhead_x2_kernel(tc, x, w1_words, w1_scales, b1, g, w_he
                 if blk + 3 < BLOCKS:
                     load_x(blk + 3)
             gelu(blk, 2)
-            mm1(blk, 5)
+            mm1(blk, 2 + ahead)
             gelu(blk, 3)
             gain_h(blk, 0)
             if prev:
                 mm2(blk - 1, 0)
                 mm2(blk - 1, 1)
-            mm1(blk, 6)
+            mm1(blk, 3 + ahead)
             if more:
                 copy_x(blk + 1, 2)
                 copy_x(blk + 1, 3)
                 quant_x(blk + 1, 1)
             quant_h(blk, 0)
             gelu(blk, 4)
-            mm1(blk, 7)
+            mm1(blk, 4 + ahead)
             if prev:
                 for tp in range(2):
                     if more:
                         abs_z2(blk - 1, tp)
                     relu_z2(blk - 1, tp)
-            for j in range(PACK):
-                weigh_u(blk // 2, PACK * (blk % 2) + j)
-            for j in range(5, 8):
+            for j in range(2):
+                weigh_u0(2 * blk + j)
+            for j in range(FEATURE_TILES - ahead, FEATURE_TILES):
                 gelu(blk, j)
                 if more:
-                    mm1(blk + 1, j - 5)
+                    mm1(blk + 1, j + ahead - FEATURE_TILES)
             if prev and more:
                 tanh_tiles(PACK * (blk - 1), PACK * blk)
-        last = BLOCKS - 1
+
         gain_h(last, 1, (0,))
         abs_z2(last - 1, 0)
         abs_z2(last - 1, 1)
         tanh_tiles(PACK * (last - 1), PACK * last)
-        for tile in range(2):
-            turn_u(tile)
+        u0_ps = bank(U_BANK, "u0_ps")
+        for t in range(2):
+            turn_u0(u0_ps, t)
         gain_h(last, 1, (1,))
         for tp in range(2):
             quant_h(last, 1, (tp,))
@@ -374,52 +380,50 @@ def tile_attractordepthbinhead_x2_kernel(tc, x, w1_words, w1_scales, b1, g, w_he
             relu_z2(last, tp)
         tanh_tiles(PACK * last, PACK * last + 2)
         tanh_tiles(PACK * last + 2, TILES)
-        for tile in range(2, 2 * PACK):
-            turn_u(tile)
+        for t in range(2, PACK):
+            turn_u0(u0_ps, t)
+        for j in range(FEATURE_TILES):
+            wide_u(j)
+
         ln_tiles(0, 1)
         finish_y(0, 1)
         for k in range(SHIFTS):
-            make_dx(0, k)
+            make_d(0, k)
         ln_tiles(1, PACK)
-        sum_u(1)
+        pick_u(0)
         finish_y(1, PACK)
-        sum_u(0)
+        nc.vector.tensor_reduce(out=u_sum[:, 0:PACK], in_=u0_ps[:].rearrange("p (t f) -> p t f", t=PACK), axis=mybir.AxisListType.X, op=ALU.add)
         for blk in range(1, BLOCKS):
             ln_tiles(PACK * blk, PACK * (blk + 1))
         nc.scalar.activation(out=half_lc[:], in_=lower[:], func=ACT.Ln, scale=1.0 / TRIALS)
-
-        logits_next = 0
         for blk in range(1, BLOCKS):
             finish_y(PACK * blk, PACK * (blk + 1))
-        nc.vector.scalar_tensor_tensor(out=half_lc[:], in0=lower[:], scalar=-1.0 / TEMP, in1=half_lc[:], op0=ALU.mult, op1=ALU.mult)
+        nc.vector.scalar_tensor_tensor(out=half_lc[:], in0=lower[:], scalar=-1.0 / TEMPERATURE, in1=half_lc[:], op0=ALU.mult, op1=ALU.mult)
         nc.vector.tensor_tensor(out=lc[:], in0=half_lc[:], in1=half_lc[:, ::-1], op=ALU.add)
-        for k in range(CHUNKS + 7):
-            for c in range(SHIFTS):
-                if k + 1 < CHUNKS:
-                    make_dx(k + 1, c)
-                if 0 <= k - 6 < CHUNKS:
-                    reduce_e(k - 6, c)
-                if (SHIFTS * k + c) % 6 == 0 and (SHIFTS * k + c) // 6 < 4 * FT:
-                    wide_u((SHIFTS * k + c) // 6)
-            if k < CHUNKS:
-                square_dx(k)
-            if 0 <= k - 1 < CHUNKS:
-                rsqrt(k - 1)
-            if 0 <= k - 2 < CHUNKS:
-                weigh(k - 2)
-            if 0 <= k - 3 < CHUNKS:
-                square_e(k - 3)
-            if 0 <= k - 4 < CHUNKS:
-                fold_e(k - 4)
-            if k >= 7 and (k - 7) % 4 == 3:
-                centres((k - 7) // 4)
-            if k == 48:
-                k_ps = psum.tile([P, BINS], F32, tag="bank%d" % U_BANKS[last], name="k_ps")
-                nc.tensor.transpose(k_ps[:], kcol[:], ident[:])
-                slopes()
-            if k > 49 and logits_next < TILES:
-                make_logits(logits_next)
-                logits_next += 1
+
+        for step in range(CHUNKS + CENTRE_LAG):
+            for k in range(SHIFTS):
+                if step + 1 < CHUNKS:
+                    make_d(step + 1, k)
+                if 0 <= step - REDUCE_LAG < CHUNKS:
+                    reduce_e(step - REDUCE_LAG, k)
+                for index in range(WOVEN):
+                    if WIDE_AT[index] == SHIFTS * step + k:
+                        wide_u(FEATURE_TILES + index)
+            for stage, lag in ((square_dx, 0), (rsqrt, RSQRT_LAG), (weigh, WEIGH_LAG), (square_e, SQUARE_LAG)):
+                if 0 <= step - lag < CHUNKS:
+                    stage(step - lag)
+            if step >= CENTRE_LAG and (step - CENTRE_LAG) % PARTS == PARTS - 1:
+                centres((step - CENTRE_LAG) // PARTS)
+            for duo in range(1, DUOS):
+                if WIDE_AT[FEATURE_TILES * duo - 1] // SHIFTS == step:
+                    pick_u(duo)
+            if step == SLOPES_STEP:
+                slopes(0, TILES - 2)
+            if step == LAST_SLOPES_STEP:
+                slopes(TILES - 2, TILES)
+            if 0 <= step - FIRST_LOGITS_STEP < TILES:
+                make_logits(step - FIRST_LOGITS_STEP)
 
         rounded = {}
 
@@ -436,11 +440,11 @@ def tile_attractordepthbinhead_x2_kernel(tc, x, w1_words, w1_scales, b1, g, w_he
             for tile in range(PACK * blk, PACK * (blk + 1)):
                 nc.vector.scalar_tensor_tensor(out=res[:, tile, :], in0=res[:, tile, :], scalar=norm[:, tile:tile + 1], in1=logit[:, tile, :], op0=ALU.mult, op1=ALU.mult)
             nc.sync.dma_start(out=out_0[BLOCK * blk:BLOCK * (blk + 1), :].rearrange("(p t) m -> p t m", t=PACK), in_=res[:, tiles_of(blk), :])
-            rounded[blk] = work.tile([P, BINS * PACK], BF16, tag="rounded", bufs=4, name="rounded%d" % blk, align_bytes=64)
+            rounded[blk] = work.tile([P, BINS * PACK], BF16, tag="rounded", bufs=BLOCKS, name="rounded%d" % blk, align_bytes=64)
             nc.scalar.copy(out=rounded[blk][:].rearrange("p (m t) -> p m t", t=PACK), in_=res[:, tiles_of(blk), :].rearrange("p t m -> p m t"))
 
         def planes(blk):
-            codes = work.tile([P, BINS], U32, tag="codes", bufs=4, name="codes%d" % blk, align_bytes=64)
+            codes = work.tile([P, BINS], U32, tag="codes", bufs=BLOCKS, name="codes%d" % blk, align_bytes=64)
             nc.vector.quantize_mx(out=codes[:].bitcast(FP8X4), scales=out_scales[:, blk, :], in_=rounded[blk][:])
             nc.sync.dma_start(out=out_1[blk].rearrange("p m t -> p (m t)").bitcast(I32), in_=codes[:].bitcast(I32))
 
@@ -449,13 +453,13 @@ def tile_attractordepthbinhead_x2_kernel(tc, x, w1_words, w1_scales, b1, g, w_he
         scale_total(0)
         invert_total(0)
         for blk in range(BLOCKS):
-            if blk + 1 < BLOCKS:
+            if blk < last:
                 scale_total(blk + 1)
             finish(blk)
-            if blk + 1 < BLOCKS:
+            if blk < last:
                 invert_total(blk + 1)
             if blk > 0:
                 planes(blk - 1)
         planes(last)
-        for q in range(4):
+        for q in range(QUADRANTS):
             nc.scalar.dma_start(out=out_2.bitcast(I32)[:, 4 * q:4 * q + 4, :].rearrange("g r m -> r g m"), in_=out_scales[32 * q:32 * q + 4].bitcast(I32))

import math
from contextlib import ExitStack

import concourse.mybir as mybir
from concourse.masks import make_identity

F32 = mybir.dt.float32
BF16 = mybir.dt.bfloat16
I32 = mybir.dt.int32
U32 = mybir.dt.uint32
U8 = mybir.dt.uint8
FP8X4 = mybir.dt.float8_e4m3fn_x4
FP4X4 = mybir.dt.float4_e2m1fn_x4
ACT = mybir.ActivationFunctionType
ALU = mybir.AluOpType

P = 128
TOKENS, E, F, BINS = 2048, 1024, 1024, 128
GROUPS, MEMBERS = 8, 16
PACK = 4
BLOCK = P * PACK
BLOCKS = TOKENS // BLOCK
TILES = TOKENS // P
PASSES = E // BLOCK
FEATURE_TILES = F // P
QUADRANTS = 4
SHIFTS = 4
PARTS = MEMBERS // SHIFTS
CHUNKS = TILES * PARTS
BETA = 1.0 / math.sqrt(2.0)
EPS = 1e-6
TEMPERATURE = 20.0
TRIALS = BINS - 1
FLOPS = 2 * TOKENS * E * F + 2 * TOKENS * F * 2 * BINS

X_BANKS = (0, 1)
MM1_BANKS = (2, 3, 4)
MM2_BANKS = (5, 6)
U_BANK = 7
D_BANKS = (0, 1, 2, 3, 4)
SUM_BANKS = (5, 6)
FIRST_WIDE_BANK = D_BANKS[-1]

WARM_UP_MATMULS = 5
SCALAR_SQUARE_EVERY = 4
RSQRT_LAG, WEIGH_LAG, SQUARE_LAG, REDUCE_LAG, CENTRE_LAG = 1, 2, 3, 6, 7

DUOS = 2 * (BLOCKS - 1)
WOVEN = (DUOS - 1) * FEATURE_TILES
EARLY_WIDE_AT = [0, 5, 10, 15, 15, 15, 15]
WIDE_AT = EARLY_WIDE_AT + [21 + 13 * s // 2 for s in range(WOVEN - len(EARLY_WIDE_AT))]
PLAIN_FROM_CHUNK = 60
PLAIN_SHIFTS = ((0, 3), (2,), (1,), (0,))
SLOPES_STEP, LAST_SLOPES_STEP, FIRST_LOGITS_STEP = 48, 60, 50


def tile_attractordepthbinhead_x2_kernel(tc, x, w1_words, w1_scales, b1, g, w_head_words, w_head_scales, w_q, out_0, out_1, out_2):
    nc = tc.nc
    with ExitStack() as ctx:
        keep = ctx.enter_context(tc.tile_pool(name="keep", bufs=1))
        work = ctx.enter_context(tc.tile_pool(name="work", bufs=2))
        psum = ctx.enter_context(tc.psum_pool(name="psum", bufs=1))
        ctx.enter_context(tc.manual_schedule())

        def bank(b, name, width=BLOCK):
            return psum.tile([P, width], F32, tag="bank%d" % b, name=name)

        w1_raw = keep.tile([P, PASSES, 2 * F], U8, align_bytes=64)
        s1_raw = keep.tile([P, PASSES, F], U8, align_bytes=64)
        wh = keep.tile([P, PASSES, 4 * BINS], U8, align_bytes=64)
        sh = keep.tile([P, PASSES, 2 * BINS], U8, align_bytes=64)
        zeros = keep.tile([P, BLOCK], BF16)
        nc.vector.memset(s1_raw[:].bitcast(I32), 0)
        nc.vector.memset(zeros[:], 0.0)
        nc.vector.memset(sh[:].bitcast(I32), 0)

        x_raw = {}

        def load_x(blk):
            x_raw[blk] = work.tile([P, PACK, E], BF16, tag="x_raw", name="x_raw%d" % blk)
            rows = x[blk * BLOCK:(blk + 1) * BLOCK, :].rearrange("(p t) e -> p t e", t=PACK)
            for kp in range(PASSES):
                nc.sync.dma_start(out=x_raw[blk][:, :, BLOCK * kp:BLOCK * (kp + 1)], in_=rows[:, :, BLOCK * kp:BLOCK * (kp + 1)])

        def load_scales(queue, plane, rows):
            for q in range(QUADRANTS):
                queue.dma_start(out=plane[32 * q:32 * q + 4].bitcast(I32), in_=rows.bitcast(I32)[:, 4 * q:4 * q + 4, :].rearrange("g r n -> r g n"))

        nc.sync.dma_start(out=w1_raw[:].bitcast(I32), in_=w1_words.bitcast(I32).rearrange("g p n -> p g n"))
        load_x(0)
        load_scales(nc.scalar, s1_raw, w1_scales)
        warm = keep.tile([P, 1], F32)
        nc.scalar.activation(out=warm[:], in_=zeros[:, 0:1], func=ACT.Gelu)
        vec = {}
        for name, src in (("b1", b1), ("g", g), ("wq", w_q)):
            vec[name] = keep.tile([P, PASSES, PACK], BF16, name="vec_" + name)
            nc.sync.dma_start(out=vec[name][:], in_=src.rearrange("(a p t) -> p a t", a=PASSES, t=PACK))
        load_x(1)
        nc.sync.dma_start(out=wh[:].bitcast(I32), in_=w_head_words.bitcast(I32).rearrange("g p n -> p g n"))
        load_scales(nc.sync, sh, w_head_scales)

        ident = keep.tile([P, P], F32)
        make_identity(nc, ident[:])
        kvec = keep.tile([P, BINS], F32)
        nc.gpsimd.iota(kvec[:], pattern=[[1, BINS]], base=0, channel_multiplier=0, allow_small_or_imprecise_dtypes=True)
        lower = keep.tile([P, BINS], F32)
        nc.gpsimd.tensor_scalar(out=lower[:], in0=kvec[:], scalar1=EPS, scalar2=1.0, op0=ALU.add, op1=ALU.mult)
        gw = keep.tile([P, FEATURE_TILES], F32)
        half_lc = keep.tile([P, BINS], F32)
        lc = keep.tile([P, BINS], F32)
        warm_ps = bank(U_BANK, "warm_ps")
        for k in range(WARM_UP_MATMULS):
            nc.tensor.matmul(out=warm_ps[:], lhsT=zeros[:, 0:P], rhs=zeros[:], start=True, stop=True)

        w1p = keep.tile([P, PASSES, 2 * F], U8, align_bytes=64)
        s1p = keep.tile([P, PASSES, F], U8, align_bytes=64)

        def permute_w1(a):
            for kp in range(PASSES):
                nc.vector.tensor_copy(
                    out=w1p[:, kp, 2 * BLOCK * a:2 * BLOCK * (a + 1)].rearrange("p (t m b) -> p t m b", t=PACK, b=2),
                    in_=w1_raw[:, kp, 2 * BLOCK * a:2 * BLOCK * (a + 1)].rearrange("p (m t b) -> p t m b", t=PACK, b=2))
            nc.vector.tensor_copy(
                out=s1p[:, :, BLOCK * a:BLOCK * (a + 1)].rearrange("p g (t m) -> p g t m", t=PACK),
                in_=s1_raw[:, :, BLOCK * a:BLOCK * (a + 1)].rearrange("p g (m t) -> p g t m", t=PACK))

        gel = keep.tile([P, BLOCKS, FEATURE_TILES, BLOCK], F32)
        soft = keep.tile([P, TILES, 2, BINS], F32)
        relu = keep.tile([P, TILES, 2, BINS], F32)
        ytab = keep.tile([P, TILES, 3, BINS], F32)
        logit = keep.tile([P, TILES, BINS], F32)
        res = keep.tile([P, TILES, BINS], F32)
        slope = keep.tile([P, TILES], F32)
        shift = keep.tile([P, TILES], F32)
        total = keep.tile([P, TILES], F32)
        norm = keep.tile([P, TILES], F32)
        out_scales = keep.tile([P, BLOCKS, BINS], U8, align_bytes=64)
        u_sum = keep.tile([P, TILES], F32)
        xt, xg, xq, xs, z1, hg, hq, hs, z2, u_wide = {}, {}, {}, {}, {}, {}, {}, {}, {}, {}

        def turn_x(blk, b, banks=X_BANKS):
            kp, tp = divmod(b, 2)
            xt[blk, b] = bank(banks[b % len(banks)], "xt%d_%d" % (blk, b))
            words = x_raw[blk][:].bitcast(F32)
            for t in range(2):
                for u in range(2):
                    col = (2 * t + u) * P
                    nc.tensor.transpose(xt[blk, b][:, col:col + P], words[:, 2 * tp + t, 2 * P * kp + u:2 * P * (kp + 1):2], ident[:])

        def copy_x(blk, b):
            kp, tp = divmod(b, 2)
            if tp == 0:
                xg[blk, kp] = work.tile([P, BLOCK * PACK], BF16, tag="xg", name="xg%d_%d" % (blk, kp), align_bytes=64)
            dst = xg[blk, kp][:].bitcast(F32)[:, BLOCK * tp:BLOCK * (tp + 1)]
            nc.scalar.copy(out=dst.rearrange("p (t r u) -> p t r u", t=2, u=2), in_=xt[blk, b][:].rearrange("p (t u r) -> p t r u", t=2, u=2))

        def quant_x(blk, kp):
            xq[blk, kp] = work.tile([P, BLOCK], U32, tag="xq", bufs=2 * PASSES, name="xq%d_%d" % (blk, kp), align_bytes=64)
            xs[blk, kp] = work.tile([P, BLOCK], U8, tag="xs", bufs=2 * PASSES, name="xs%d_%d" % (blk, kp), align_bytes=64)
            nc.vector.quantize_mx(out=xq[blk, kp][:].bitcast(FP8X4), scales=xs[blk, kp][:], in_=xg[blk, kp][:])

        def mm1(blk, j):
            z1[blk, j] = bank(MM1_BANKS[(FEATURE_TILES * blk + j) % len(MM1_BANKS)], "z1_%d_%d" % (blk, j))
            for kp in range(PASSES):
                nc.tensor.matmul_mx(out=z1[blk, j][:], lhsT=w1p[:, kp, 2 * P * j:2 * P * (j + 1)].bitcast(FP4X4), lhsT_scale=s1p[:, kp, P * j:P * (j + 1)],
                                    rhs=xq[blk, kp][:].bitcast(FP8X4), rhs_scale=xs[blk, kp][:], start=(kp == 0), stop=(kp == PASSES - 1))

        def gelu(blk, j):
            nc.scalar.activation(out=gel[:, blk, j, :], in_=z1[blk, j][:], func=ACT.Gelu, bias=vec["b1"][:, j // PACK, j % PACK:j % PACK + 1])

        def gain_h(blk, a, tps=(0, 1)):
            if tps[0] == 0:
                hg[blk, a] = work.tile([P, BLOCK * PACK], BF16, tag="hg", name="hg%d_%d" % (blk, a), align_bytes=64)
            lo, hi = 2 * P * tps[0], 2 * P * (tps[-1] + 1)
            nc.vector.tensor_tensor(
                out=hg[blk, a][:, PACK * lo:PACK * hi].rearrange("p (n t) -> p n t", t=PACK),
                in0=gel[:, blk, PACK * a:PACK * (a + 1), lo:hi].rearrange("p t n -> p n t"),
                in1=vec["g"][:, a, :].unsqueeze(1).to_broadcast([P, hi - lo, PACK]), op=ALU.mult)

        def quant_h(blk, a, tps=(0, 1)):
            if tps[0] == 0:
                hq[blk, a] = work.tile([P, BLOCK], U32, tag="hq", bufs=PASSES + 1, name="hq%d_%d" % (blk, a), align_bytes=64)
                hs[blk, a] = work.tile([P, BLOCK], U8, tag="hs", bufs=PASSES + 1, name="hs%d_%d" % (blk, a), align_bytes=64)
            lo, hi = 2 * P * tps[0], 2 * P * (tps[-1] + 1)
            nc.vector.quantize_mx(out=hq[blk, a][:, lo:hi].bitcast(FP8X4), scales=hs[blk, a][:, lo:hi], in_=hg[blk, a][:, PACK * lo:PACK * hi])

        def mm2(blk, tp):
            z2[blk, tp] = bank(MM2_BANKS[tp], "z2_%d_%d" % (blk, tp))
            for t in range(2):
                tok = slice(P * (2 * tp + t), P * (2 * tp + t + 1))
                for hf in range(2):
                    col = (2 * t + hf) * BINS
                    for a in range(PASSES):
                        nc.tensor.matmul_mx(out=z2[blk, tp][:, col:col + BINS], lhsT=hq[blk, a][:, tok].bitcast(FP8X4), lhsT_scale=hs[blk, a][:, tok],
                                            rhs=wh[:, a, 2 * BINS * hf:2 * BINS * (hf + 1)].bitcast(FP4X4), rhs_scale=sh[:, a, BINS * hf:BINS * (hf + 1)],
                                            start=(a == 0), stop=(a == PASSES - 1))

        def by_member(tiles):
            return tiles.rearrange("p t h (i q) -> p (t h) i q", q=GROUPS)

        def z2_by_member(blk, tp):
            return z2[blk, tp][:].rearrange("p (s q i) -> p s i q", q=GROUPS, i=MEMBERS)

        def abs_z2(blk, tp):
            first = PACK * blk + 2 * tp
            nc.scalar.activation(out=by_member(soft[:, first:first + 2]), in_=z2_by_member(blk, tp), func=ACT.Abs)

        def relu_z2(blk, tp):
            first = PACK * blk + 2 * tp
            nc.vector.tensor_scalar(out=by_member(relu[:, first:first + 2]), in0=z2_by_member(blk, tp), scalar1=0.0, scalar2=None, op0=ALU.max)

        def soft_tiles(lo, hi):
            return soft[:, lo:hi].rearrange("p t h m -> p (t h m)")

        def tanh_tiles(lo, hi):
            nc.scalar.activation(out=soft_tiles(lo, hi), in_=soft_tiles(lo, hi), func=ACT.Tanh, scale=0.5)

        def ln_tiles(lo, hi):
            nc.scalar.activation(out=soft_tiles(lo, hi), in_=soft_tiles(lo, hi), func=ACT.Ln, scale=0.5, bias=0.5)

        def finish_y(lo, hi):
            nc.vector.scalar_tensor_tensor(out=ytab[:, lo:hi, 0, :], in0=soft[:, lo:hi, 0, :], scalar=BETA, in1=relu[:, lo:hi, 0, :], op0=ALU.add, op1=ALU.subtract)
            nc.vector.tensor_tensor(out=ytab[:, lo:hi, 1:3, :], in0=relu[:, lo:hi, 1:2, :].to_broadcast([P, hi - lo, 2, BINS]),
                                    in1=soft[:, lo:hi, 1:2, :].to_broadcast([P, hi - lo, 2, BINS]), op=ALU.subtract)

        def weigh_u0(j):
            nc.vector.tensor_scalar(out=gel[:, 0, j, :], in0=gel[:, 0, j, :], scalar1=gw[:, j:j + 1], scalar2=None, op0=ALU.mult)

        def turn_u0(u0_ps, t):
            for j in range(FEATURE_TILES):
                nc.tensor.matmul(out=u0_ps[:, P * t:P * (t + 1)], lhsT=gel[:, 0, j, P * t:P * (t + 1)], rhs=ident[:],
                                 start=(j == 0), stop=(j == FEATURE_TILES - 1), is_transpose=True)

        def wide_u(index):
            duo, j = divmod(index, FEATURE_TILES)
            blk, tp = 1 + duo // 2, duo % 2
            if j == 0:
                u_wide[duo] = bank(FIRST_WIDE_BANK if duo == 0 else U_BANK, "u_wide%d" % duo, 2 * P)
            nc.tensor.matmul(out=u_wide[duo][:], lhsT=gw[:, j:j + 1].to_broadcast([P, P]), rhs=gel[:, blk, j, 2 * P * tp:2 * P * (tp + 1)],
                             start=(j == 0), stop=(j == FEATURE_TILES - 1))

        def pick_u(duo):
            for t in range(2):
                tile = PACK + 2 * duo + t
                masked = work.tile([P, P], F32, tag="masked", name="masked%d" % tile)
                nc.vector.scalar_tensor_tensor(out=masked[:], in0=u_wide[duo][:, P * t:P * (t + 1)], scalar=1.0, in1=ident[:], op0=ALU.mult, op1=ALU.mult,
                                               accum_out=u_sum[:, tile:tile + 1])

        d_ps, chunk, chunk_pair, acc = {}, {}, {}, {}

        def make_d(n, k):
            tile, part = divmod(n, PARTS)
            if k == 0:
                d_ps[n] = bank(D_BANKS[n % len(D_BANKS)], "d%d" % n)
            row = ytab[:, tile].rearrange("p s m -> p (s m)")
            start = BINS + GROUPS * (SHIFTS * part + k)
            plain = n >= PLAIN_FROM_CHUNK and k in PLAIN_SHIFTS[n % len(PLAIN_SHIFTS)]
            nc.tensor.matmul(out=d_ps[n][:, P * k:P * (k + 1)], lhsT=row[:, start:start + BINS], rhs=ident[:], start=True, stop=False, is_transpose=True)
            nc.tensor.matmul(out=d_ps[n][:, P * k:P * (k + 1)], lhsT=row[:, 0:BINS], rhs=ident[:], start=False, stop=True, is_transpose=not plain)

        def square_dx(n):
            if n % 2 == 0:
                chunk_pair[n // 2] = work.tile([P, 2, BLOCK], F32, tag="pair", bufs=5, name="pair%d" % n)
            chunk[n] = chunk_pair[n // 2][:, n % 2, :]
            nc.scalar.activation(out=chunk[n], in_=d_ps[n][:], func=ACT.Square, bias=-BETA)

        def rsqrt(n):
            nc.scalar.activation(out=chunk[n], in_=chunk[n], func=ACT.Abs_reciprocal_sqrt, scale=2.0, bias=1.0)

        def weigh(n):
            nc.vector.tensor_tensor(out=chunk[n], in0=d_ps[n][:], in1=chunk[n], op=ALU.mult)

        def square_e(n):
            shared = (n // 2) % SCALAR_SQUARE_EVERY == 1
            if n % 2 == 0:
                if shared:
                    nc.scalar.activation(out=chunk[n], in_=chunk[n], func=ACT.Square)
            else:
                span = chunk[n] if shared else chunk_pair[n // 2][:].rearrange("p d c -> p (d c)")
                nc.vector.tensor_tensor(out=span, in0=span, in1=span, op=ALU.mult)

        def reduce_e(n, k):
            tile, part = divmod(n, PARTS)
            s = SHIFTS * part + k
            if s == 0:
                acc[tile] = bank(SUM_BANKS[tile % 2], "acc%d" % tile, BINS)
            nc.tensor.matmul(out=acc[tile][:], lhsT=chunk[n][:, P * k:P * (k + 1)], rhs=ident[:], start=(s == 0), stop=(s == MEMBERS - 1), is_transpose=True)

        def centres(tile):
            nc.vector.scalar_tensor_tensor(out=res[:, tile, :].rearrange("p (q i) -> p q i", i=MEMBERS), in0=acc[tile][:].rearrange("p (i q) -> p q i", q=GROUPS),
                                           scalar=2.0 * BETA / MEMBERS, in1=ytab[:, tile, 0, :].rearrange("p (i q) -> p q i", q=GROUPS), op0=ALU.mult, op1=ALU.subtract)

        def slopes(lo, hi):
            nc.vector.tensor_scalar(out=slope[:, lo:hi], in0=u_sum[:, lo:hi], scalar1=1.0 / TEMPERATURE, scalar2=None, op0=ALU.mult)
            nc.vector.tensor_scalar(out=shift[:, lo:hi], in0=slope[:, lo:hi], scalar1=0.0, scalar2=-float(TRIALS), op0=ALU.max, op1=ALU.mult)

        def make_logits(tile):
            nc.vector.scalar_tensor_tensor(out=logit[:, tile, :], in0=kvec[:], scalar=slope[:, tile:tile + 1], in1=lc[:], op0=ALU.mult, op1=ALU.add)

        def exp_tile(tile):
            nc.scalar.activation(out=logit[:, tile, :], in_=logit[:, tile, :], func=ACT.Exp, bias=shift[:, tile:tile + 1], accum_out=total[:, tile:tile + 1])

        ahead = len(MM1_BANKS)
        last = BLOCKS - 1
        permute_w1(0)
        for b in range(2 * PASSES):
            turn_x(0, b, X_BANKS + MM2_BANKS)
        load_x(2)
        for b in range(2 * PASSES):
            copy_x(0, b)
            if b % 2 == 1:
                quant_x(0, b // 2)
        permute_w1(1)
        nc.vector.tensor_tensor(out=gw[:], in0=vec["g"][:].rearrange("p a t -> p (a t)"), in1=vec["wq"][:].rearrange("p a t -> p (a t)"), op=ALU.mult)
        for j in range(ahead):
            mm1(0, j)
        for blk in range(BLOCKS):
            more, prev = blk < last, blk > 0
            if prev:
                gain_h(blk - 1, 1)
            if more:
                turn_x(blk + 1, 0)
                turn_x(blk + 1, 1)
            for j in (0, 1):
                gelu(blk, j)
                mm1(blk, j + ahead)
            if more:
                copy_x(blk + 1, 0)
                copy_x(blk + 1, 1)
                quant_x(blk + 1, 0)
            if prev:
                quant_h(blk - 1, 1)
            if more:
                turn_x(blk + 1, 2)
                turn_x(blk + 1, 3)
                if blk + 3 < BLOCKS:
                    load_x(blk + 3)
            gelu(blk, 2)
            mm1(blk, 2 + ahead)
            gelu(blk, 3)
            gain_h(blk, 0)
            if prev:
                mm2(blk - 1, 0)
                mm2(blk - 1, 1)
            mm1(blk, 3 + ahead)
            if more:
                copy_x(blk + 1, 2)
                copy_x(blk + 1, 3)
                quant_x(blk + 1, 1)
            quant_h(blk, 0)
            gelu(blk, 4)
            mm1(blk, 4 + ahead)
            if prev:
                for tp in range(2):
                    if more:
                        abs_z2(blk - 1, tp)
                    relu_z2(blk - 1, tp)
            for j in range(2):
                weigh_u0(2 * blk + j)
            for j in range(FEATURE_TILES - ahead, FEATURE_TILES):
                gelu(blk, j)
                if more:
                    mm1(blk + 1, j + ahead - FEATURE_TILES)
            if prev and more:
                tanh_tiles(PACK * (blk - 1), PACK * blk)

        gain_h(last, 1, (0,))
        abs_z2(last - 1, 0)
        abs_z2(last - 1, 1)
        tanh_tiles(PACK * (last - 1), PACK * last)
        u0_ps = bank(U_BANK, "u0_ps")
        for t in range(2):
            turn_u0(u0_ps, t)
        gain_h(last, 1, (1,))
        for tp in range(2):
            quant_h(last, 1, (tp,))
            mm2(last, tp)
        for tp in range(2):
            abs_z2(last, tp)
            relu_z2(last, tp)
        tanh_tiles(PACK * last, PACK * last + 2)
        tanh_tiles(PACK * last + 2, TILES)
        for t in range(2, PACK):
            turn_u0(u0_ps, t)
        for j in range(FEATURE_TILES):
            wide_u(j)

        ln_tiles(0, 1)
        finish_y(0, 1)
        for k in range(SHIFTS):
            make_d(0, k)
        ln_tiles(1, PACK)
        pick_u(0)
        finish_y(1, PACK)
        nc.vector.tensor_reduce(out=u_sum[:, 0:PACK], in_=u0_ps[:].rearrange("p (t f) -> p t f", t=PACK), axis=mybir.AxisListType.X, op=ALU.add)
        for blk in range(1, BLOCKS):
            ln_tiles(PACK * blk, PACK * (blk + 1))
        nc.scalar.activation(out=half_lc[:], in_=lower[:], func=ACT.Ln, scale=1.0 / TRIALS)
        for blk in range(1, BLOCKS):
            finish_y(PACK * blk, PACK * (blk + 1))
        nc.vector.scalar_tensor_tensor(out=half_lc[:], in0=lower[:], scalar=-1.0 / TEMPERATURE, in1=half_lc[:], op0=ALU.mult, op1=ALU.mult)
        nc.vector.tensor_tensor(out=lc[:], in0=half_lc[:], in1=half_lc[:, ::-1], op=ALU.add)

        for step in range(CHUNKS + CENTRE_LAG):
            for k in range(SHIFTS):
                if step + 1 < CHUNKS:
                    make_d(step + 1, k)
                if 0 <= step - REDUCE_LAG < CHUNKS:
                    reduce_e(step - REDUCE_LAG, k)
                for index in range(WOVEN):
                    if WIDE_AT[index] == SHIFTS * step + k:
                        wide_u(FEATURE_TILES + index)
            for stage, lag in ((square_dx, 0), (rsqrt, RSQRT_LAG), (weigh, WEIGH_LAG), (square_e, SQUARE_LAG)):
                if 0 <= step - lag < CHUNKS:
                    stage(step - lag)
            if step >= CENTRE_LAG and (step - CENTRE_LAG) % PARTS == PARTS - 1:
                centres((step - CENTRE_LAG) // PARTS)
            for duo in range(1, DUOS):
                if WIDE_AT[FEATURE_TILES * duo - 1] // SHIFTS == step:
                    pick_u(duo)
            if step == SLOPES_STEP:
                slopes(0, TILES - 2)
            if step == LAST_SLOPES_STEP:
                slopes(TILES - 2, TILES)
            if 0 <= step - FIRST_LOGITS_STEP < TILES:
                make_logits(step - FIRST_LOGITS_STEP)

        rounded = {}

        def tiles_of(blk):
            return slice(PACK * blk, PACK * (blk + 1))

        def scale_total(blk):
            nc.vector.tensor_scalar(out=total[:, tiles_of(blk)], in0=total[:, tiles_of(blk)], scalar1=1.0 / BINS, scalar2=None, op0=ALU.mult)

        def invert_total(blk):
            nc.vector.reciprocal(out=norm[:, tiles_of(blk)], in_=total[:, tiles_of(blk)])

        def finish(blk):
            for tile in range(PACK * blk, PACK * (blk + 1)):
                nc.vector.scalar_tensor_tensor(out=res[:, tile, :], in0=res[:, tile, :], scalar=norm[:, tile:tile + 1], in1=logit[:, tile, :], op0=ALU.mult, op1=ALU.mult)
            nc.sync.dma_start(out=out_0[BLOCK * blk:BLOCK * (blk + 1), :].rearrange("(p t) m -> p t m", t=PACK), in_=res[:, tiles_of(blk), :])
            rounded[blk] = work.tile([P, BINS * PACK], BF16, tag="rounded", bufs=BLOCKS, name="rounded%d" % blk, align_bytes=64)
            nc.scalar.copy(out=rounded[blk][:].rearrange("p (m t) -> p m t", t=PACK), in_=res[:, tiles_of(blk), :].rearrange("p t m -> p m t"))

        def planes(blk):
            codes = work.tile([P, BINS], U32, tag="codes", bufs=BLOCKS, name="codes%d" % blk, align_bytes=64)
            nc.vector.quantize_mx(out=codes[:].bitcast(FP8X4), scales=out_scales[:, blk, :], in_=rounded[blk][:])
            nc.sync.dma_start(out=out_1[blk].rearrange("p m t -> p (m t)").bitcast(I32), in_=codes[:].bitcast(I32))

        for tile in range(TILES):
            exp_tile(tile)
        scale_total(0)
        invert_total(0)
        for blk in range(BLOCKS):
            if blk < last:
                scale_total(blk + 1)
            finish(blk)
            if blk < last:
                invert_total(blk + 1)
            if blk > 0:
                planes(blk - 1)
        planes(last)
        for q in range(QUADRANTS):
            nc.scalar.dma_start(out=out_2.bitcast(I32)[:, 4 * q:4 * q + 4, :].rearrange("g r m -> r g m"), in_=out_scales[32 * q:32 * q + 4].bitcast(I32))
